import numpy as np, ml_dtypes
CORES = [2,3,42,43,82,83,122,123]
N = 8
BF = ml_dtypes.bfloat16
def gentries(a):
    return np.ascontiguousarray(a.reshape(8, 16, -1).transpose(0, 2, 1)).reshape(8, -1)
def gtable(e):
    e = np.asarray(e); return np.ascontiguousarray(e.reshape(8, -1, 16).transpose(0, 2, 1)).reshape(128, -1).astype(np.int32)
V, X, SW, RO, CAP = 768, 128, 2, 2, 56
E = (N - 1) * X
Q = 4 ** SW
def base(rng, top):
    b = rng.integers(top // 10, top * 9 // 10, (N, 8, 1, V))
    debt = np.clip(b + rng.integers(-(top // 16), top // 16 + 1, (N, 8, 16, V)), 1, top)
    c = rng.integers(1, top // 5 + 1, (N, 8, 1, 4 * V)); few = rng.random((N, 8, 1, 4 * V)) < 0.5
    coll = np.where(few, 0, np.clip(c + rng.integers(-16, 17, (N, 8, 16, 4 * V)), 0, top // 5))
    o = np.argsort(rng.random((N, 8, 4 * V)), axis=-1)
    rest = np.concatenate([o[..., E:], np.broadcast_to(4 * V + np.arange(E), (N, 8, E))], axis=-1)
    sg = np.take_along_axis(rest, np.argsort(rng.random((N, 8, 4 * V)), axis=-1), 2)
    return {"cash": rng.integers(0, top // 8 + 1, (N, 8, 16, V)), "debt": debt, "coll": coll, "sg": sg, "xp": np.ascontiguousarray(o[..., :E]),
            "th": Q + rng.integers(0, Q // 4 + 1, (N, 8, 16)), "val": real(rng, 0)}
def real(rng, w):
    s = np.exp2(rng.integers(-w, w + 1, (N, 8, 1, V)))
    return (s * (0.5 + rng.random((N, 8, 16, V)))).astype(np.float32)
def lay(rng, S, C, F, at=None):
    S = np.asarray(S, np.int64).reshape(-1); C = np.asarray(C, np.int64).reshape(-1); F = np.asarray(F, np.int64).reshape(-1)
    left = rng.permutation(np.setdiff1d(np.arange(4 * V), np.concatenate([C, F]))); m = E - len(F)
    x = np.full(E, -1, np.int64); x[rng.permutation(E)[:len(F)] if at is None else at] = F; x[x < 0] = left[:m]
    s = np.full(4 * V, -1, np.int64); s[S] = C
    s[s < 0] = rng.permutation(np.concatenate([left[m:], np.setdiff1d(4 * V + np.arange(E), C)]))
    return s, x
def four_of(b):
    return (4 * np.asarray(b, np.int64)[:, None] + np.arange(4)).reshape(-1)
def pack(d):
    return {"cash": d["cash"].reshape(N, 128, V).astype(np.int32), "debt": d["debt"].reshape(N, 128, V).astype(np.int32),
            "coll": d["coll"].reshape(N, 128, 4 * V).astype(np.float32).astype(BF), "sig": np.stack([gtable(a) for a in d["sg"]]),
            "xpt": np.stack([gtable(a) for a in d["xp"]]), "th": d["th"].reshape(N, 128, 1).astype(np.int32), "val": np.ascontiguousarray(d["val"].reshape(N, 128, V)).astype(np.float32)}
def setup_inputs(rng):
    return pack(base(rng, 1000))
def setup_inputs_spread(rng):
    d = base(rng, 1000); one = (N, 8, 1, V); full = (N, 8, 16, V)
    b = np.where(rng.random(one) < 0.5, np.exp2(10 * rng.random(one)), 1 + 1023 * rng.random(one))
    d["debt"] = np.clip((b * (0.75 + 0.5 * rng.random(full))).astype(np.int64), 1, 1023)
    d["cash"] = np.clip((np.exp2(10 * rng.random(one) ** 2) * rng.random(full)).astype(np.int64), 0, 1023)
    c = np.exp2(8 * rng.random((N, 8, 1, 4 * V))) * (rng.random((N, 8, 1, 4 * V)) < 0.5)
    d["coll"] = np.clip((c * rng.random((N, 8, 16, 4 * V))).astype(np.int64), 0, 255)
    d["th"] = Q + (SW * Q * rng.random((N, 8, 16)) ** 4).astype(np.int64)
    d["val"] = 32.0 * real(rng, 1)
    return pack(d)
def setup_inputs_ends(rng):
    d = base(rng, 1000); full = (N, 8, 16, V)
    z = np.where(rng.random((N, 8, 1, V)) < 0.5, rng.random((N, 8, 1, V)), rng.random(full))
    d["cash"] = np.where(z < 0.8, 0, 1023); d["debt"] = np.where((z < 0.6) | (z > 0.87), 1023, 1)
    c = np.where(rng.random((N, 8, 1, 4 * V)) < 0.5, rng.random((N, 8, 1, 4 * V)), rng.random((N, 8, 16, 4 * V)))
    d["coll"] = np.where(c < 0.25, 255, 0)
    d["val"] = np.where(rng.random(full) < 0.75, 128.0, 8.0)
    n = rng.choice(np.array([0, 8, 9, 16]), (N, 8, 1)); n[:, 0] = 16; n[:, 1] = 9; n[:, 2] = 8; n[:, 7] = 0
    d["th"] = np.where(np.argsort(rng.random((N, 8, 16)), axis=-1) < n, Q, Q * (1 + SW))
    slots = [np.concatenate([np.array([0, E - 1]), 1 + rng.permutation(E - 2)[:8 * RO - 2]]) for j in range(4)]
    top = np.concatenate([4 * np.array([0, 1, V // 4 - 2, V // 4 - 1]) + 3 - t for t in range(RO)])
    b = 4 * np.arange(V // 4); inner = b[(4 * b >= E // 2) & (4 * b + 3 < 4 * V - (E - E // 2))]
    for q in range(N):
        for g in range(8):
            at = slots[(g - 1) // 2]; S = []; C = []; T = []; hold = []; i = 0; k = 4 * RO
            if g % 2:
                more = rng.permutation(b); feed = (4 * top[:, None] + np.arange(2)).reshape(-1); F = feed + 2; T.append(top); hold.append(four_of(top))
            else:
                more = rng.permutation(inner); feed = 4 * V + at; F = np.concatenate([np.arange(E // 2), np.arange(4 * V - (E - E // 2), 4 * V)])
            for j in range(SW):
                nxt = more[i:i + k]; i += k; k *= 2
                S.append((4 * nxt[:, None] + np.arange(2)).reshape(-1)); C.append(feed); feed = four_of(nxt)
                T.append(nxt); hold.append((4 * nxt[:, None] + np.arange(2, 4)).reshape(-1))
            T = np.concatenate(T); hold = np.concatenate(hold); leak = more[i:i + len(hold) // 4]
            S.append(hold); C.append(four_of(leak))
            d["sg"][q, g], d["xp"][q, g] = lay(rng, np.concatenate(S), np.concatenate(C), F, at if g % 2 else None)
            d["cash"][q, g][:, T] = 0; d["debt"][q, g][:, T] = 1023; d["coll"][q, g][:, four_of(T)] = 0; d["val"][q, g][:, T] = 128.0
            d["cash"][q, g][:, leak] = 0; d["debt"][q, g][:, leak] = 1
    return pack(d)
def setup_inputs_corners(rng):
    d = base(rng, 600); d["debt"] = d["debt"] & -4
    d["val"] = ((2 ** 16 + rng.integers(0, 2 ** 14, (N, 8, 16, V)) + 0.4921875) * 2.0 ** -20).astype(np.float32)
    d["th"][:] = Q; d["th"][:, 3::4] = Q * (1 + SW)
    for q in range(N):
        for g in range(8):
            cash, debt, coll = d["cash"][q, g], d["debt"][q, g], d["coll"][q, g]
            S = []; C = []; F = []; vs = []; h = 4 * rng.permutation(V // 4)
            for t in range(RO):
                i = np.sort(np.concatenate([np.array([0]), 1 + rng.permutation(V // 4 - 2)[:10], np.array([V // 4 - 1])]))
                v = 4 * i + 3 - t; u = h[8 * t:8 * t + 8]; vs.append(v)
                S += [4 * v[1] + 1, 4 * v[2] + 1, 4 * u[0] + 2, 4 * u[1], 4 * u[1] + 3, 4 * v[5] + 2, 4 * u[2] + 1, 4 * u[3] + 1, 4 * u[4] + 1, 4 * u[5] + 1, 4 * v[9] + 3 if g % 2 == 0 else 4 * u[6]]
                C += [4 * v[j] for j in (0, 1, 2, 3, 4, 5, 7, 8, 9, 10, 11)]; F.append(4 * v[6])
            o1, o2, leak = h[32], h[33], h[34]
            S += [4 * o1 + j for j in range(4)] + [4 * o2 + j for j in range(4)]
            C += [4 * o1, 4 * o1 + 1, 4 * o1 + 2, 4 * leak, 4 * o2, 4 * o2 + 1, 4 * o2 + 2, 4 * o1 + 3]
            d["sg"][q, g], d["xp"][q, g] = lay(rng, S, C, F)
            if g % 2:
                s = d["sg"][q, g]; own = np.flatnonzero((s < 4 * V) & (rng.random(4 * V) < 0.25))
                coll[:, own] = (debt[:, s[own] >> 2] >> 2) - rng.integers(0, 2, (16, len(own)))
            for v in vs:
                cash[:, v] = 0; debt[:, v] = 1023
                cash[rng.permutation(16)[:8], v[7]] = 1023; cash[rng.permutation(16)[:7], v[8]] = 1023
                coll[:, 4 * v[9] + np.arange(4)] = 200; coll[:, 4 * v[10] + np.arange(4)] = np.array([0, 0, 0, 200])
            b = h[24:32]; c = rng.integers(0, 21, (16, 8))
            cash[:, b] = c; debt[:, b] = 800 + c + rng.integers(0, 2, (16, 8)); coll[:, four_of(b)] = 200
            cash[:, h[32:35]] = 0; debt[:, h[32:34]] = 1023; debt[:, leak] = 1; coll[:, four_of(h[32:34])] = 0
    return pack(d)
def setup_inputs_crowd(rng):
    d = base(rng, 600); d["th"][:] = Q; d["th"][:, 3] = Q + rng.integers(0, Q // 4 + 1, (N, 16)); n = V // 32
    for q in range(N):
        for g in range(8):
            cash, debt, coll = d["cash"][q, g], d["debt"][q, g], d["coll"][q, g]; h = 4 * rng.permutation(V // 4); S = []; C = []; lane = rng.permutation(16)
            for t in range(RO):
                v = 4 * rng.permutation(V // 4)[:4 * n] + 3 - t; w = h[t * n:(t + 1) * n]
                S.append(four_of(w)); C.append(4 * v)
                cash[:, v] = 0; debt[:, v] = 1023
                coll[:, 4 * v] = 0; coll[:, 4 * v + 1] = 200; coll[:, 4 * v + 2] = 200; coll[:, 4 * v + 3] = 0; coll[lane[0], 4 * v + 1] = 0
                if g % 2: cash[lane[1], v] = 1023
                cash[:, v.reshape(n, 4)[::2, 3]] = 1023
            d["sg"][q, g], d["xp"][q, g] = lay(rng, np.concatenate(S), np.concatenate(C), [])
    return pack(d)
def setup_inputs_calm(rng):
    d = base(rng, 600)
    n = 9 + rng.integers(0, 8, (N, 8, 1)); d["th"] = np.where(np.argsort(rng.random((N, 8, 16)), axis=-1) < n, Q, Q + rng.integers(0, SW * Q + 1, (N, 8, 16)))
    for q in range(N):
        for g in range(8):
            cash, debt, coll = d["cash"][q, g], d["debt"][q, g], d["coll"][q, g]; h = 4 * rng.permutation(V // 4); S = []; C = []; at = 0
            for t in range(RO):
                k = (g + q + t) % 4 if g < 6 else (0 if t < RO - 1 else V // 4 - (g - 6))
                i = 4 * rng.permutation(V // 4) + 3 - t; v = i[:k]; rest = i[k:]; w = h[at:at + k]; at += k
                m = np.argsort(rng.random((16, len(rest))), axis=0) < 8
                cash[:, rest] = np.where(m, 1023, cash[:, rest])
                c = rng.integers(0, 21, (16, k)); cash[:, v] = c; debt[:, v] = 800 + c + CAP + rng.integers(0, 2, (16, k)); coll[:, four_of(v)] = 200
                S += [4 * w + 3, 4 * v + 1, 4 * v + 2]; C += [4 * v, 4 * w + 1, 4 * w + 2]
                if g >= 6 and t == RO - 1:
                    z = np.concatenate([4 * v, 4 * w])[:E]; S.append(z); C.append(4 * V + rng.permutation(E)[:len(z)])
            d["sg"][q, g], d["xp"][q, g] = lay(rng, np.concatenate(S), np.concatenate(C), [])
    return pack(d)
def check_ranges(d):
    bad = []
    for k, lo, hi in (("cash", 0, 1023), ("debt", 1, 1023), ("coll", 0, 255), ("sig", 0, 4 * V + E - 1), ("xpt", 0, 4 * V - 1), ("th", Q, Q * (1 + SW))):
        a = np.asarray(d[k]).astype(np.float64)
        if not (np.min(a) >= lo and np.max(a) <= hi): bad.append("range of " + k)
        elif np.any(a != np.floor(a)): bad.append("whole numbers of " + k)
    x = np.asarray(d["val"]).astype(np.float64)
    if not (np.min(x) >= 2.0 ** -4 and np.max(x) <= 128): bad.append("range of val")
    elif np.max(x) > 16 * np.min(x): bad.append("uneven sizes of val")
    for q in range(N):
        both = np.sort(np.concatenate([gentries(np.asarray(d["sig"][q])), gentries(np.asarray(d["xpt"][q]))], axis=1), axis=1)
        if np.any(both != np.arange(4 * V + E)[None, :]): bad.append("sig and xpt of rank " + str(q) + " are not every number once")
    return bad
def take(a, i):
    return np.take_along_axis(a, i[:, :, None, :], 3)
def four(y):
    return ((y[..., 0::4] + y[..., 1::4]) + y[..., 2::4]) + y[..., 3::4]
def forth(a):
    out = np.empty_like(a)
    for q in range(N):
        for d in range(1, N):
            b = slice((d - 1) * X, d * X); out[(q + d) % N, :, :, b] = np.roll(a[q, :, :, b], 1, axis=0)
    return out
def home(a):
    out = np.empty_like(a)
    for q in range(N):
        for d in range(1, N):
            b = slice((d - 1) * X, d * X); out[q, :, :, b] = np.roll(a[(q + d) % N, :, :, b], -1, axis=0)
    return out
def clear(e, L, c, sg, xp):
    at = np.where(sg < 4 * V, sg >> 2, sg - 3 * V); p = L
    for k in range(SW):
        y = np.maximum(0.25 * take(np.concatenate([p, forth(take(p, xp >> 2))], axis=3), at), c)
        p = np.minimum(L, e + four(y))
    return p, p < L, y > c
def inverse(sg, xp):
    inv = np.zeros((N, 8, 4 * V + E), np.int64)
    np.put_along_axis(inv, sg, np.arange(4 * V)[None, None, :], 2); np.put_along_axis(inv, xp, 4 * V + np.arange(E)[None, None, :], 2)
    return inv
def threat(D, M, inv, a):
    m = np.where(D, a, 0.0)
    for k in range(SW):
        c = np.where(M, np.repeat(m, 4, axis=3), 0.0)
        z = take(np.concatenate([c, home(take(c, inv[:, :, 4 * V:]))], axis=3), inv[:, :, :4 * V])
        m = np.where(D, a + 0.25 * four(z), 0.0)
    return m
def novate(t, m, M, e, sg, inv, lim):
    v = np.arange(3 - t, V, 4); votes = np.sum(Q * m[..., v] >= lim, axis=2)
    s = inv[:, :, 4 * v]; w = s >> 2; act = (votes >= 9) & (s < 4 * V) & (w != v)
    k = np.argmax(np.sum(~M.reshape(N, 8, 16, V, 4)[:, :, :, v], axis=2), axis=3)
    low = np.full((N, 8, V), V, np.int64); r, g, i = np.nonzero(act)
    low[r, g, v[i]] = v[i]; np.minimum.at(low, (r, g, w[r, g, i]), v[i])
    ok = (low[r, g, v[i]] == v[i]) & (low[r, g, w[r, g, i]] == v[i])
    r, g, i = r[ok], g[ok], i[ok]; e = np.array(e); sg = np.array(sg)
    e[r, g, :, v[i]] += CAP
    a = 4 * v[i] + k[r, g, i]; b = 4 * w[r, g, i] + k[r, g, i]
    sg[r, g, a], sg[r, g, b] = sg[r, g, b], sg[r, g, a]
    return e, sg
def reference(cash, debt, coll, sig, xpt, th, val):
    e = cash.astype(np.float64).reshape(N, 8, 16, V); L = debt.astype(np.float64).reshape(N, 8, 16, V)
    c = coll.astype(np.float32).astype(np.float64).reshape(N, 8, 16, 4 * V); lim = th.astype(np.float64).reshape(N, 8, 16, 1)
    sg = np.stack([gentries(a) for a in sig]).astype(np.int64); xp = np.stack([gentries(a) for a in xpt]).astype(np.int64)
    for t in range(RO):
        p, D, M = clear(e, L, c, sg, xp); inv = inverse(sg, xp)
        e, sg = novate(t, threat(D, M, inv, 1.0), M, e, sg, inv, lim)
    p, D, M = clear(e, L, c, sg, xp)
    m = threat(D, M, inverse(sg, xp), val.astype(np.float64).reshape(N, 8, 16, V))
    return {"pay": p.reshape(N, 128, V).astype(np.float32), "mu": m.reshape(N, 128, V).astype(np.float32)}

def check_inputs(d):
    bad = list(check_ranges(d))
    if not bad:
        for name, y in reference(**d).items():
            for q in range(N):
                v = np.abs(np.asarray(y[q], np.float64)); s = np.sqrt(np.mean(v * v))
                if v.max() > 7 * s or s < 2.0 ** -5: bad.append('%s of rank %d is uneven or too small' % (name, q))
    return bad

@@ -1,0 +1,663 @@
+from concourse.bass import DstId, RemoteDMATransfer
+from concourse.mybir import AluOpType as A, ActivationFunctionType as F
+
+V, X, NR = 768, 128, 8
+C = 4 * V
+E = (NR - 1) * X
+Z = 192
+NV = 512
+SV = 768
+NB = 416
+f32, bf, i32, u16, f16 = "float32", "bfloat16", "int32", "uint16", "float16"
+
+
+def sb(n, d):
+    return ("sbuf", [128, n], d)
+
+
+SCRATCH = {
+    "xs": sb(248, i32), "dbt": sb(V, i32), "csh": sb(V, i32), "col": sb(C, bf), "v4": sb(V, f32), "nv": sb(V, f32), "thi": sb(4, i32),
+    "io": sb(512, f32), "W32": sb(256, f32), "Wb": sb(256, bf), "Wh": sb(256, f16), "Wq": sb(256, f16), "Un": sb(128, bf), "Gb": sb(2048, bf),
+    "Fm": sb(512, bf), "Am": sb(512, f32), "Bm": sb(512, f32), "Em": sb(512, f32), "Rm": sb(128, f32), "B32": sb(128, f32), "Bb": sb(128, bf),
+    "one": sb(128, f32), "pi": sb(8, i32), "pp": sb(16, f32), "kq": sb(Z, f32), "cX": sb(NV, bf), "dum": sb(12, f32),
+    "c5": sb(384, bf), "Wq32": sb(128, f32), "Dn": sb(128, f16), "Un32": sb(128, f32), "of6": sb(72, f32), "Yq": sb(84, f32),
+    "sigr": sb(Z + C, f32), "invr": sb(Z + C + E, f32), "Cx": sb(Z + C + E, bf), "S1": sb(Z + V, f32),
+    "Dw": sb(C + E, f32), "Lq": sb(V + E, f32), "Lqc": sb(V, f16), "p1h": sb(V, f16), "nH": sb(V, f32), "K": sb(V, bf),
+    "rh": sb(C, f16), "r32": sb(C - 4 * NV, f32), "nD": sb(V, bf), "df": sb(E, bf), "z32": sb(C + E - SV, f32), "zb": sb(C, bf),
+    "c0": sb(C + E, bf), "Tw": sb(V + E, bf), "Ts": sb(V, bf), "t32": sb(V, f32), "wa": sb(C + E, f32), "wb": sb(C + E, f32),
+    "za": sb(V, bf), "z2": sb(V, bf), "nvt": sb(Z, bf), "a12": sb(2 * Z, bf), "aw": sb(C, bf), "blk": sb(2 * V + Z, bf), "eff": sb(2 * Z, bf),
+    "sA": sb(E, f16), "sB": sb(E, f16), "sC": sb(E, bf), "sD": sb(E, bf), "lA": sb(E, f16), "lB0": sb(E, f16), "lB1": sb(E, f16),
+    "ia": sb(248, i32), "ib": sb(248, i32), "ic": sb(248, i32), "fa": sb(248, f32), "fb": sb(248, f32), "fc": sb(Z, f32),
+    "qu": sb(248, u16), "xbu": sb(56, u16), "atu": sb(Z, u16), "sigu": sb(Z, u16), "invu": sb(248, u16), "bsl": sb(56, u16), "plu": sb(NB // 4, u16),
+    "mk": sb(Z, f32), "asku": sb(48, u16), "qbu": sb(48, u16), "lvu": sb(48, u16), "blu": sb(108, u16), "L96": sb(108, f32), "lw": sb(48, i32),
+    "X0": sb(144, f32), "X1": sb(240, f32), "thr": sb(60, f32), "km": sb(48, f32), "Y": sb(120, f32), "Yu": sb(120, u16),
+    "of": sb(84, f32), "ofu": sb(84, u16), "vs": sb(2 * Z, f32), "vi": sb(2 * Z, f32), "vc": sb(2 * Z, bf), "cp": sb(2 * Z, f32),
+    "x1": sb(2 * Z, f32), "x2": sb(2 * Z, f32), "nS": sb(Z, f32),
+}
+for _b in range(8):
+    SCRATCH["P%d" % _b] = ("psum", [128, 512], f32)
+ALIAS = {"lwr": ("z32", V), "msg": ("blk", V), "G32": ("wa", 2048), "PL": ("wb", 2048), "s32a": ("Lq", E), "s32b": ("Dw", E), "acc": ("r32", 2 * NB)}
+NX = 10
+SEMAPHORES = ["qv", "qs", "qt", "qg"] + ["ar%d" % x for x in range(NX)] + ["ls%d" % x for x in range(NX)] + ["d%d" % x for x in range(30)]
+
+
+def b(name, c0=0, c1=None, st=1, p=None):
+    if name in ALIAS:
+        return (ALIAS[name][0], c0, ALIAS[name][1] if c1 is None else c1, st, p, None)
+    return (name, c0, SCRATCH[name][1][1] if c1 is None else c1, st, p, None)
+
+
+def ind(win, off):
+    return win[:5] + (off,)
+
+
+def rank_program(g, core, T, topo):
+    rank = T.rank_of(core)
+    if rank is None:
+        return
+    eng = {"v": g.vector, "s": g.scalar, "t": g.tensor, "g": g, "y": g.sync}
+    cnt = {"qv": 0, "qs": 0, "qt": 0, "qg": 0}
+    seen = {q: {} for q in eng}
+    clock = {}
+    hist = {}
+    nd = [0]
+    ends = []
+
+    def ap(o):
+        if not isinstance(o, tuple):
+            return o
+        ps = slice(None) if o[4] is None else slice(*o[4])
+        a = T[o[0]][ps, o[1]:o[2]] if o[3] == 1 else T[o[0]][ps, o[1]:o[2]:o[3]]
+        return a if o[5] is None else a.indirect(ap(o[5]))
+
+    def wait(q, tok):
+        if seen[q].get(tok[0], 0) >= tok[1]:
+            return
+        eng[q].wait_ge(T.sem[tok[0]], tok[1])
+        seen[q][tok[0]] = tok[1]
+        for s, n in clock.get(tok, {}).items():
+            if seen[q].get(s, 0) < n:
+                seen[q][s] = n
+
+    def span(o):
+        return (0, 512, 1) if SCRATCH[o[0]][0] == "psum" else (o[1], o[2], o[3])
+
+    def deps(q, cq, reads, writes):
+        need = {}
+        for o, wr in [(o, False) for o in reads] + [(o, True) for o in writes]:
+            lo, hi, st = span(o)
+            ps = SCRATCH[o[0]][0] == "psum"
+            for c0, c1, s1, w, qq, tok in hist.get(o[0], []):
+                if c0 >= hi or lo >= c1 or not (w or wr or (ps and qq != cq)):
+                    continue
+                if qq is not None and cq is not None:
+                    if qq == cq == "t":
+                        continue
+                    if st == s1 and (lo - c0) % st:
+                        continue
+                need[tok[0]] = max(need.get(tok[0], 0), tok[1])
+        for s, n in need.items():
+            wait(q, (s, n))
+
+    def note(q, cq, reads, writes, tok):
+        clock[tok] = dict(seen[q])
+        for o in writes:
+            hist.setdefault(o[0], []).append(span(o) + (True, cq, tok))
+        for o in reads:
+            hist.setdefault(o[0], []).append(span(o) + (False, cq, tok))
+
+    def emit(q, fn, out, ins):
+        reads = [o for o in ins if isinstance(o, tuple)]
+        reads += [o[5] for o in reads + [out] if o[5] is not None]
+        deps(q, q, reads, [out])
+        s = "q" + q
+        cnt[s] += 1
+        fn().then_inc(T.sem[s], 1)
+        note(q, q, reads, [out], (s, cnt[s]))
+
+    def cp(o, i):
+        emit("v", lambda: g.vector.tensor_copy(ap(o), ap(i)), o, [i])
+
+    def tt(o, x, y, op):
+        emit("v", lambda: g.vector.tensor_tensor(ap(o), ap(x), ap(y), op), o, [x, y])
+
+    def ts(o, x, s1, op0, s2=None, op1=None):
+        if op1 is None:
+            emit("v", lambda: g.vector.tensor_scalar(ap(o), ap(x), ap(s1), None, op0), o, [x, s1])
+        else:
+            emit("v", lambda: g.vector.tensor_scalar(ap(o), ap(x), ap(s1), ap(s2), op0, op1), o, [x, s1, s2])
+
+    def ms(o, c):
+        emit("v", lambda: g.vector.memset(ap(o), c), o, [])
+
+    def act(o, i, fn=F.Identity, bias=None, scale=None):
+        kw = {}
+        if bias is not None:
+            kw["bias"] = bias
+        if scale is not None:
+            kw["scale"] = scale
+        emit("s", lambda: g.scalar.activation(ap(o), ap(i), fn, **kw), o, [i])
+
+    def mm(o, l, r, start, stop):
+        emit("t", lambda: g.tensor.matmul(ap(o), ap(l), ap(r), start, stop), o, [l, r])
+
+    def iota(o, pat, base, cm):
+        if SCRATCH[o[0]][2] == i32:
+            emit("g", lambda: g.iota(ap(o), pat, base, cm), o, [])
+        else:
+            emit("g", lambda: g.iota(ap(o), pat, base, cm, allow_small_or_imprecise_dtypes=True), o, [])
+
+    def asel(o, i, pat, base, cm, op=A.is_equal):
+        emit("g", lambda: g.affine_select(ap(o), ap(i), pat, op, 0.0, base, cm), o, [i])
+
+    def dma(q, pairs):
+        s = "d%d" % nd[0]
+        nd[0] += 1
+        rd = [i for o, i in pairs if isinstance(i, tuple)]
+        wr = [o for o, i in pairs if isinstance(o, tuple)]
+        deps(q, None, rd, wr)
+        for o, i in pairs:
+            eng[q].dma_start(ap(o), ap(i)).then_inc(T.sem[s], 16)
+        tok = (s, 16 * len(pairs))
+        note(q, None, rd, wr, tok)
+        ends.append(tok)
+
+    def plan(r, sign):
+        c = T.cores[r]
+        dst = [(r + sign * (j + 1)) % NR for j in range(NR - 1)]
+        near = [j for j in range(NR - 1) if topo.chip(T.cores[dst[j]]) == topo.chip(c)]
+        first = list(range(4)) if min(near) >= 4 else list(range(3, 7))
+        calls = []
+        for part in (first, [j for j in range(NR - 1) if j not in first]):
+            far = [j for j in part if j not in near]
+            en = topo.engines(c, T.cores[dst[far[0]]])
+            w = len(en) // len(far)
+            row = [(j, dst[j], sum(1 << e for e in en[i * w:(i + 1) * w])) for i, j in enumerate(far)]
+            for j in part:
+                if j in near:
+                    row.append((j, dst[j], sum(1 << e for e in topo.engines(c, T.cores[dst[j]]) if e not in en)))
+            calls.append((min(part) * X, (max(part) + 1) * X, row))
+        return calls
+
+    nx = [0]
+    landed = [None]
+
+    def exchange(sign, src, land, l0, make):
+        x = nx[0]
+        nx[0] += 1
+        sent = 0
+        for c0, c1, row in plan(rank, sign):
+            make(c0, c1)
+            deps("g", None, [b(src, c0, c1)], [])
+            trs = []
+            for j, d, m in row:
+                rid, pid, _ = topo.addr(T.cores[d])
+                trs.append(RemoteDMATransfer(dst_ids=[DstId(rid=rid, pnc=pid)], dma_engine_mask=m, remote_sem=T.sem["ar%d" % x],
+                                             src=ap(b(src, j * X, (j + 1) * X)), dst=T[land][:, l0 + j * X:l0 + (j + 1) * X]))
+                sent += bin(m).count("1")
+            g.remote_dma_fused(trs, local_sem=T.sem["ls%d" % x])
+        note("g", None, [b(src)], [], ("ls%d" % x, sent))
+        ends.append(("ls%d" % x, sent))
+        got = sum(bin(m).count("1") for r in range(NR) if r != rank for _, _, row in plan(r, sign) for j, d, m in row if d == rank)
+        tok = ("ar%d" % x, got)
+        clock[tok] = {}
+        landed[0] = tok
+        hist.setdefault(land, []).append((l0, l0 + E, 1, True, None, tok))
+
+    def mat(name, kind):
+        c = {"I": 0, "D": 16, "U": 112}[kind]
+        return b(name, c, c + 128)
+
+    def m4(name, h):
+        return b(name, 128 * h, 128 * h + 128)
+
+    def col(j):
+        return b("pp", j, j + 1)
+
+    def P(k, c0=0, c1=512, st=1):
+        return b("P%d" % k, c0, c1, st)
+
+    def gat(win, lst, c0, c1):
+        return ind(win, b(lst, c0 // 16, c1 // 16))
+
+    ROW = (0, 128, 18)
+    halves = ((0, 448), (448, 896))
+    vb = ((0, NV), (NV, V))
+    GP = [[256, 16], [-16, 8], [-257, 16]]
+
+    def spread(dst, src):
+        wait("y", landed[0])
+        dma("y", [(b(dst, Z, None, 1, (i, 128, 16)), src) for i in range(16)])
+
+    def round_matrices(t):
+        o = 4 * (3 - t)
+        for h in range(4):
+            asel(m4("Am", h), b("one"), [[-16, 8], [256, 4], [-1, 4]], -o - 256 * h, 1)
+            asel(m4("Bm", h), b("one"), [[-16, 8], [256, 4], [0, 4]], -o - 256 * h, 1)
+        asel(b("Rm"), b("one"), [[-16, 8], [0, 16]], -o, 1)
+
+    dma("y", [(b("xs", Z, 248), T.xpt[:])])
+    dma("s", [(b("dbt"), T.debt[:])])
+    dma("y", [(b("xs", 0, Z), T.sig[:])])
+    dma("s", [(b("csh"), T.cash[:])])
+    dma("y", [(b("col"), T.coll[:])])
+    iota(b("pi", 0, 1), [[0, 1]], 0, 1)
+    iota(b("io"), [[1, 512]], 0, 0)
+    ms(b("W32"), 1.0)
+    ms(b("fb"), 0.0)
+    ms(b("one"), 1.0)
+    ms(b("B32"), 4.0)
+    asel(b("W32"), b("W32"), [[0, 2], [-1, 128]], 0, 1)
+    dma("y", [(b("invr", Z, None, 1, ROW), b("fb")), (b("wb", 0, None, 1, ROW), b("fb"))])
+    dma("y", [(b("thi", 0, 1), T.th[:])])
+    NS = C + E - SV
+    iota(b("z32", NS - 1024, NS), [[1, 1024]], 64 + C + E - 1024, 0)
+    for c0 in range(0, NS - 1024, 512):
+        n = min(512, NS - 1024 - c0)
+        act(b("z32", c0, c0 + n), b("io", 0, n), bias=float(64 + SV + c0))
+    act(b("Wb"), b("W32"))
+    p0 = b("pi", 0, 1)
+    ts(b("pi", 1, 2), p0, 3, A.bitwise_and)
+    ts(b("pi", 2, 3), p0, 2, A.arith_shift_right, 3, A.bitwise_and)
+    ts(b("pi", 3, 4), p0, 15, A.bitwise_and)
+    cp(b("pp", 1, 4), b("pi", 1, 4))
+    for t in range(2):
+        ts(col(9 + t), col(2), 16.0, A.mult, 13.0 - 4 * t, A.add)
+    ts(col(5), col(3), -float(Z), A.add, 1.0 / 8192, A.mult)
+    ts(col(4), col(1), 192.0, A.mult)
+    ts(col(8), col(1), 192.0, A.mult, col(2), A.add)
+    ts(b("ic", Z, 248), b("xs", Z, 248), 2, A.arith_shift_right)
+    cp(b("xbu"), b("ic", Z, 248))
+    ts(b("ia"), b("xs"), 4, A.arith_shift_right)
+    ts(b("ib"), b("xs"), 248.0, A.mult)
+    ts(b("ia"), b("ia"), -3967.0, A.mult)
+    tt(b("ia"), b("ia"), b("ib"), A.add)
+    cp(b("qu"), b("ia"))
+    act(ind(b("wb"), b("qu", SV // 16, 248)), b("z32", 0, NS), F.Silu)
+    act(b("Un"), mat("W32", "U"), scale=-1.0)
+    act(b("Un32"), mat("W32", "U"), scale=-1.0)
+    act(b("Wq32"), mat("W32", "I"), scale=0.25)
+    exchange(1, "sA", "lA", 0, lambda c0, c1: ts(b("sA", c0, c1), gat(b("dbt"), "xbu", c0, c1), -512.0, A.add))
+    iota(b("c5"), [[0, 384]], -512, 0)
+    asel(b("B32"), b("B32"), [[-16, 8], [0, 16]], 0, 1, A.is_ge)
+    asel(b("B32"), b("B32"), [[16, 8], [0, 16]], 15, -1, A.is_ge)
+    for h in range(4):
+        asel(m4("Fm", h), b("B32"), [[0, 8], [1, 4], [0, 4]], -h, 0)
+    asel(b("Rm"), b("one"), [[-16, 8], [0, 4], [-4, 4]], 0, 1, A.is_ge)
+    asel(b("Rm"), b("Rm"), [[16, 8], [0, 4], [4, 4]], 3, -1, A.is_ge)
+    for h in range(4):
+        asel(m4("Em", h), b("Rm"), [[0, 8], [1, 4], [0, 4]], -h, 0)
+    iota(b("K"), [[0, V]], 0, 0)
+    iota(b("cX"), [[0, NV]], -128, 0)
+    iota(b("kq"), [[1, 4], [0, 48]], 0, 0)
+    round_matrices(0)
+    wait("y", landed[0])
+    dma("y", [(b("v4"), T.val[:]), (b("nv", 0, None, 1, (0, 112)), T.val[16:128, :]), (b("nv", 0, None, 1, (112, 128)), T.val[0:16, :])])
+    ts(b("Wq"), b("W32"), 0.25, A.mult)
+    ts(b("ic", 0, Z), b("xs", 0, Z), 2, A.arith_shift_right)
+    ts(b("ib", 0, Z), b("xs", 0, Z), -2304.0, A.add)
+    cp(b("t32"), b("csh"))
+    tt(b("ib", 0, Z), b("ib", 0, Z), b("ic", 0, Z), A.max)
+    ts(b("Lq", 0, V), b("dbt"), 0.25, A.mult)
+    cp(b("atu"), b("ib", 0, Z))
+    cp(b("Wh"), b("W32"))
+    for c0 in range(0, SV, 512):
+        n = min(512, SV - c0)
+        ts(gat(b("invr", Z), "qu", c0, c0 + n), b("io", 0, n), 1.0, A.mult, float(64 + c0), A.add)
+    dma("y", [(b("fa"), b("invr", Z, None, 1, ROW))])
+    dma("y", [(b("fb"), b("wb", 0, None, 1, ROW))])
+
+    for j in range(2):
+        mm(P(4 + j, 0, 384), mat("W32", "I"), b("t32", 384 * j, 384 * j + 384), True, False)
+        mm(P(4 + j, 0, 384), mat("Wb", "I"), b("c5"), False, False)
+    for j, (c0, c1) in enumerate(vb):
+        mm(P(6 + j, 0, c1 - c0), mat("W32", "I"), b("t32", c0, c1), True, False)
+        for k in range(4):
+            mm(P(6 + j, 0, c1 - c0), mat("Wb", "I"), b("col", 4 * c0 + k, 4 * c1, 4), False, k == 3)
+        act(b("nH", c0, c1), P(6 + j, 0, c1 - c0), bias=0.0 if j == 0 else -512.0)
+    for j, (c0, c1) in enumerate(halves):
+        mm(P(j, 0, 448), mat("Wq", "U"), b("lA", c0, c1), True, True)
+        ts(b("Lq", V + c0, V + c1), P(j, 0, 448), 128.0, A.add)
+    for j in range(4):
+        tt(b("rh", 768 * j, 768 * j + 768), gat(b("Lq"), "atu", 768 * j, 768 * j + 768), b("col", 768 * j, 768 * j + 768), A.max)
+        for k in range(4):
+            mm(P(4 + j // 2, Z * (j % 2), Z * (j % 2) + Z), mat("Wh", "I"), b("rh", 768 * j + k, 768 * j + 768, 4), False, j % 2 == 1 and k == 3)
+        if j == 2:
+            mm(P(2, 0, 248), mat("W32", "I"), b("fa"), True, False)
+    mm(P(2, 0, 248), mat("W32", "I"), b("fb"), False, True)
+    cp(b("S1", Z, Z + 384), P(4, 0, 384))
+    cp(b("S1", Z + 384), P(5, 0, 384))
+    ts(b("qu"), P(2, 0, 248), -63.75, A.add, C - 0.75, A.min)
+
+    def open_sums():
+        for j, (c0, c1) in enumerate(vb):
+            mm(P(4 + j, 0, c1 - c0), mat("W32", "D"), b("nH", c0, c1), True, False)
+            mm(P(4 + j, 0, c1 - c0), b("Dn"), b("Lqc", c0, c1), False, False)
+            mm(P(4 + j, 0, c1 - c0), mat("Wb", "D"), b("K", c0, c1), False, False)
+
+    def first_lists():
+        act(b("Cx", Z, Z + 1536), gat(b("col"), "qu", 0, 1536), scale=-1.0)
+        act(b("fa"), P(2, 0, 248))
+        act(b("Cx", Z + 1536, Z + C), gat(b("col"), "qu", 1536, C), scale=-1.0)
+        ts(b("Lqc"), b("dbt"), -512.0, A.add)
+        for j in range(2):
+            tt(b("p1h", 384 * j, 384 * j + 384), P(4 + j, 0, 384), b("Lqc", 384 * j, 384 * j + 384), A.min)
+        ts(b("Dn"), mat("W32", "D"), -1.0, A.mult)
+        ts(b("Cx", Z + C), gat(b("col"), "qu", C, C + E), -1.0, A.mult)
+        ts(b("fc"), b("xs", 0, Z), 64.0, A.add)
+        ts(col(6), b("thi", 0, 1), -1.0, A.mult, 16.0, A.add)
+        ts(b("dum"), b("io", 0, Z, 16), 1.0 / 8192, A.mult, col(5), A.add)
+
+    def swaps():
+        tt(b("of", 0, 72), b("of6"), b("Yq", 0, 72), A.min)
+        ts(b("ofu", 0, 72), b("of", 0, 72), 8192.0, A.mult, float(Z), A.add)
+        for e in range(2):
+            act(ind(b("sigr"), b("ofu", 12 * e, 12 * e + 12)), b("vs", Z - Z * e, 2 * Z - Z * e), F.Silu)
+        dma("y", [(b("fc"), b("sigr", Z, None, 1, ROW))])
+        for e in range(2):
+            act(ind(b("invr"), b("ofu", 48 + 12 * e, 60 + 12 * e)), b("vi", Z - Z * e, 2 * Z - Z * e), F.Silu)
+        dma("y", [(b("fa"), b("invr", Z, None, 1, ROW))])
+        for e in range(2):
+            cp(ind(b("Cx"), b("ofu", 24 + 12 * e, 36 + 12 * e)), b("vc", Z - Z * e, 2 * Z - Z * e))
+        open_sums()
+        for j in range(2):
+            mm(P(6 + j, 0, 384), mat("W32", "I"), b("S1", Z + 384 * j, Z + 384 * j + 384), True, True)
+            tt(b("p1h", 384 * j, 384 * j + 384), P(6 + j, 0, 384), b("Lqc", 384 * j, 384 * j + 384), A.min)
+
+    def clear2(t):
+        close = t == 2
+        land = "lB%d" % (t % 2)
+        exchange(1, "sB", land, 0, lambda c0, c1: tt(b("sB", c0, c1), gat(b("S1", Z), "xbu", c0, c1), b("sA", c0, c1), A.min))
+        if t == 0:
+            iota(b("G32"), [[0, 2048]], 1, 0)
+            asel(b("G32"), b("G32"), GP, 0, 1)
+            first_lists()
+            spread("sigr", b("fc"))
+        else:
+            swaps()
+        if t == 1:
+            round_matrices(1)
+            iota(b("aw", 12, C, 16), [[0, Z]], 0, 0)
+        mm(P(0, 0, 384), mat("Wq", "I"), b("p1h", 0, 384), True, False)
+        mm(P(0, 0, 384), b("Un"), b("cX", 0, 384), False, True)
+        if t == 0:
+            open_sums()
+        for j, (c0, c1) in enumerate(halves):
+            mm(P(2 + j, 0, 448), mat("Wb", "D"), b("Cx", Z + C + c0, Z + C + c1), True, False)
+        mm(P(1, 0, 448), mat("Wb", "I"), b("Cx", Z + C, Z + C + 448), True, False)
+        for l in range(4):
+            tt(b("Dw", l, 1536, 4), P(0, 0, 384), b("Cx", Z + l, Z + 1536, 4), A.add)
+            mm(P(6 + l % 2, 0, 384), mat("Wq", "I"), b("p1h", 384), True, False)
+            mm(P(6 + l % 2, 0, 384), mat("Wb", "I"), b("Cx", Z + 1536 + l, Z + C, 4), False, True)
+            act(b("Dw", 1536 + l, C, 4), P(6 + l % 2, 0, 384), bias=128.0)
+        mm(P(0, 0, 448), mat("Wb", "I"), b("Cx", Z + C + 448), True, False)
+        ts(b("sigu"), b("fc"), -63.75, A.add)
+        for j, (c0, c1) in enumerate(halves):
+            mm(P(1 - j, 0, 448), mat("Wq", "U"), b(land, c0, c1), False, True)
+        ts(b("Dw", C, C + 448), P(1, 0, 448), 128.0, A.add)
+        act(b("Dw", C + 448), P(0, 0, 448), bias=128.0)
+        for j, (c0, c1) in enumerate(halves):
+            mm(P(2 + j, 0, 448), mat("Wq", "I"), b(land, c0, c1), False, True)
+        mm(P(7, 0, 56), mat("W32", "D"), b("fa", Z, 248), True, True)
+        for j in range(2):
+            ts(b("rh", 1024 * j, 1024 * j + 1024), gat(b("Dw"), "sigu", 1024 * j, 1024 * j + 1024), 0.0, A.max, -128.0, A.add)
+        for j in range(4):
+            act(b("r32", 256 * j, 256 * j + 256), gat(b("Dw"), "sigu", 4 * NV + 256 * j, 4 * NV + 256 * j + 256), F.Relu)
+            for k in range(4):
+                mm(P(5, 64 * j, 64 * j + 64), mat("W32", "D"), b("r32", 256 * j + k, 256 * j + 256, 4), False, j == 3 and k == 3)
+            if j % 2:
+                c0 = 1024 * (j // 2)
+                for k in range(4):
+                    mm(P(4, c0 // 4, c0 // 4 + 256), mat("Wh", "D"), b("rh", c0 + k, c0 + 1024, 4), False, j == 3 and k == 3)
+        ts(b("ib", 0, 56), P(7, 0, 56), 0.25, A.mult, -16.375, A.add)
+        cp(b("bsl"), b("ib", 0, 56))
+        if not close:
+            o = 4 * (3 - t)
+            ts(b("X0", 0, 48), b("io", 0, Z, 4), col(8), A.add, 192.0 * o, A.add)
+            ts(b("thr", 0, 48), b("io", 0, Z, 4), 16.0, A.mult, col(9 + t), A.add)
+            ts(b("thr", 48, 60), b("dum"), 16.0 * 8192, A.mult, float(C + o + 1), A.add)
+        sg = -1.0 if close else 1.0
+        for j, (c0, c1) in enumerate(halves):
+            act(b("df", c0, c1), P(2 + j, 0, 448), bias=128.0 * sg, scale=sg)
+        if close:
+            for j in (1, 0):
+                tt(b("t32", *vb[j]), P(4 + j, 0, vb[j][1] - vb[j][0]), b("nv", *vb[j]), A.max)
+            exchange(-1, "s32a", "wa", C, lambda c0, c1: tt(b("s32a", c0, c1), gat(b("t32"), "bsl", c0, c1), b("df", c0, c1), A.max))
+            for c0, c1, k in ((NV, V, 2), (0, NV, 3)):
+                mm(P(k, 0, c1 - c0), b("Wq32"), b("v4", c0, c1), True, True)
+            for j in range(2):
+                act(b("nD", *vb[j]), P(4 + j, 0, vb[j][1] - vb[j][0]), F.Relu, bias=512.0, scale=16384.0)
+        else:
+            act(b("nD", NV), P(5, 0, V - NV), F.Relu, bias=512.0, scale=16384.0)
+            ts(b("nD", 0, NV), P(4, 0, NV), 0.0, A.is_ge, 512.0, A.mult)
+            exchange(-1, "sC", "c0", C, lambda c0, c1: tt(b("sC", c0, c1), gat(b("nD"), "bsl", c0, c1), b("df", c0, c1), A.is_lt))
+        if t == 0:
+            iota(b("aw"), [[0, C]], 0, 0)
+            spread("invr", b("fa"))
+        if t == 1:
+            for l in range(4):
+                for r in range(4):
+                    asel(m4("PL", 4 * l + r), b("one"), [[-16, 8], [256, 4], [-4, 4]], -l - 256 * r, 1)
+        if not close:
+            wiring_sums(t)
+        ns = NV if close else 256
+        mm(P(6, 0, V - ns), mat("Wb", "U"), b("nD", ns), True, close)
+        if not close:
+            mm(P(6, 0, NV - ns), mat("Wb", "I"), b("cX", 0, NV - ns), False, True)
+            wiring(t)
+        for j, c0 in enumerate(range(0, 4 * ns, 512)):
+            mm(P(j % 2), mat("Wh", "I"), b("rh", c0, c0 + 512), True, False)
+            for k in range(4):
+                mm(P(j % 2, k, 512, 4), b("Un"), b("nD", c0 // 4, c0 // 4 + 128), False, k == 3)
+            if close:
+                act(b("c0", c0, c0 + 512), P(j % 2), F.Relu, bias=128.0 * 8192, scale=8192.0)
+            else:
+                act(b("c0", c0, c0 + 512), P(j % 2), F.Sign, bias=128.0 - 1.0 / 32)
+        if not close:
+            for i in range(16):
+                mm(P(3, 0, 48), m4("G32", i), b("lwr", i, V, 16), i == 0, i == 15)
+        ts(b("invu"), b("fa"), -63.75, A.add)
+        for k in range(4):
+            if not close:
+                tt(b("c0", 4 * ns + k, 4 * NV, 4), b("rh", 4 * ns + k, 4 * NV, 4), P(6, 0, NV - ns), A.is_gt)
+            tt(b("c0", 4 * NV + k, C, 4), b("r32", k, None, 4), P(6, NV - ns, V - ns), A.is_gt)
+
+    def wiring_sums(t):
+        act(b("x1", 0, Z), b("io", 0, Z), bias=-(4 * (3 - t) + 65.5), scale=-16.0)
+        for j, m, src in ((1, "Am", "fc"), (0, "Bm", "fa"), (2, "Am", "fa")):
+            for h in range(4):
+                mm(P(3, 48 * j, 48 * j + 48), m4(m, h), b(src, h, Z, 4), h == 0, h == 3)
+
+    def wiring(t):
+        ts(b("lvu"), P(3, 48, 96), -63.75, A.add)
+        act(b("msg"), ind(b("Dw"), b("lvu")), F.Sign, bias=-1.0 / 32)
+        mm(P(2, 0, Z), mat("W32", "I"), b("kq"), True, False)
+        for k in range(4):
+            for h in range(4):
+                mm(P(2, 48 * k, 48 * k + 48), m4("Fm", h), b("msg", 4 * h + k, V, 16), False, k == 3 and h == 3)
+        ts(b("ia", 0, 48), P(3, 0, 48), 0.25, A.mult, -16.375, A.add)
+        ts(b("ia", 48, 96), P(3, 0, 48), 0.0625, A.mult, -4.46875, A.add)
+        ts(b("ib", 0, 48), b("ia", 0, 48), 768.0, A.mult, col(4), A.add)
+        ts(b("ib", 48, 96), b("ia", 48, 96), -3071.0, A.mult)
+        cp(b("X1", 192, 240), b("ia", 0, 48))
+        tt(b("ib", 0, 48), b("ib", 0, 48), b("ib", 48, 96), A.add)
+        ts(b("X0", 48, 96), b("ib", 0, 48), float(C - 1), A.min)
+        cp(b("X0", 96, 144), b("lvu"))
+        cp(b("qbu"), b("X0", 48, 96))
+        ts(b("ic", 0, 48), P(3, 96, 144), 0.25, A.mult, -16.375, A.add)
+        ts(b("ic", 48, 96), P(3, 96, 144), -2368.0, A.add)
+        act(b("lwr"), ind(b("sigr", Z), b("qbu")), bias=-64.0)
+        tt(b("ic", 0, 48), b("ic", 0, 48), b("ic", 48, 96), A.max)
+        cp(b("asku"), b("ic", 0, 48))
+
+    def least():
+        cp(b("mk", 0, 96), P(2, 0, 96))
+        tt(b("mk", 0, 96), P(2, 96, Z), b("mk", 0, 96), A.min)
+        tt(b("mk", 0, 48), b("mk", 0, 48), b("mk", 48, 96), A.min)
+        ts(b("ia", 0, 48), b("mk", 0, 48), 64.0, A.add)
+        ts(b("ia", 0, 48), b("ia", 0, 48), 3, A.bitwise_and)
+        ts(b("km"), b("ia", 0, 48), col(1), A.is_equal)
+
+    def choices(t):
+        for j in range(3):
+            tt(b("X1", 48 * j, 48 * j + 48), b("X0", 48 * j, 48 * j + 48), b("km"), A.mult)
+        tt(b("L96", 0, 48), b("X0", 96, 144), b("thr", 0, 48), A.min)
+        cp(b("lw"), P(3, 0, 48))
+        tt(b("X1", 144, 192), b("lw"), b("km"), A.mult)
+        tt(b("L96", 48, 96), b("lw"), b("thr", 0, 48), A.min)
+        for r in range(4):
+            mm(P(0, 0, 60), m4("Em", r), b("X1", r, 240, 4), r == 0, r == 3)
+        cp(b("Yu", 0, 48), P(0, 0, 48))
+        act(b("cp"), ind(b("Cx", Z), b("Yu", 24, 48)), scale=-1.0)
+        ts(b("ib", 24, 48), P(0, 24, 48), 0.25, A.mult, -0.375, A.add)
+        ts(b("ic", 24, 48), P(0, 24, 48), -2304.0, A.add)
+        ts(b("ib", 0, 24), P(0, 24, 48), 0.0625, A.mult, -0.46875, A.add)
+        ts(b("ic", 0, 24), P(0, 24, 48), 248.0, A.mult)
+        ts(b("Y", 72, 84), P(0, 48, 60), 0.25, A.mult, float(V - 1), A.min)
+        tt(b("Y", 84, 108), b("ib", 24, 48), b("ic", 24, 48), A.max)
+        ts(b("ib", 0, 24), b("ib", 0, 24), -3967.0, A.mult)
+        tt(b("Y", 108, 120), b("ib", 24, 36), b("ic", 24, 36), A.max)
+        tt(b("L96", 96, 108), P(0, 48, 60), b("thr", 48, 60), A.min)
+        tt(b("Y", 48, 72), b("ib", 0, 24), b("ic", 0, 24), A.add)
+        cp(b("blu"), b("L96"))
+        cp(b("Yu", 48), b("Y", 48))
+        tt(b("x1"), ind(b("Lq"), b("Yu", 96, 120)), b("cp"), A.max)
+        tt(b("x2"), ind(b("Lq"), b("Yu", 84, 108)), b("cp"), A.max)
+        tt(b("x1"), b("x1"), b("x2"), A.subtract)
+        tt(b("nS"), ind(b("S1", Z), b("Yu", 72, 84)), b("x1", Z), A.add)
+        for l in range(4):
+            act(b("za", l, V, 4), b("zb", 4 * (3 - t) + l, C, 16))
+        act(b("Yq", 0, 48), P(0, 0, 48), scale=1.0 / 8192)
+        act(b("Yq", 48), b("Y", 48, 84), scale=1.0 / 8192)
+        act(b("x1", 0, Z), b("x1", 0, Z), bias=56.0)
+
+    for t in range(2):
+        o = 4 * (3 - t)
+        clear2(t)
+        least()
+        for j in range(2):
+            for e in range(2):
+                c0 = 1536 * e + 768 * j
+                if e:
+                    act(b("zb", c0, c0 + 768), gat(b("c0"), "invu", c0, c0 + 768), F.Relu)
+                else:
+                    ts(b("zb", c0, c0 + 768), gat(b("c0"), "invu", c0, c0 + 768), 0.0, A.max)
+                for k in range(4):
+                    mm(P(4 + e, Z * j, Z * j + Z), mat("Wb", "D"), b("zb", c0 + k, c0 + 768, 4), k == 0, k == 3)
+        mm(P(7, 0, Z), b("Rm"), b("fa", 0, Z), True, True)
+        mm(P(7, Z, 2 * Z), b("Rm"), b("fa", 0, Z), True, False)
+        mm(P(7, Z, 2 * Z), mat("W32", "I"), b("x1", 0, Z), False, True)
+        ts(b("Ts", 0, 384), P(4, 0, 384), -1.0, A.mult, -4.0, A.add)
+        act(b("Ts", 384), P(5, 0, 384), bias=-4.0, scale=-1.0)
+
+        def make_d(c0, c1):
+            m = (c0 + c1) // 2
+            act(b("sD", m, c1), gat(b("Ts"), "bsl", m, c1))
+            cp(b("sD", c0, m), gat(b("Ts"), "bsl", c0, m))
+        exchange(-1, "sD", "Tw", V, make_d)
+        if t == 0:
+            asel(b("Gb"), b("G32"), GP, 0, 1)
+            act(b("Bb"), b("B32"))
+        for j in range(2):
+            mm(P(1 + j, 0, 384), mat("Wb", "U"), b("Ts", 384 * j, 384 * j + 384), True, True)
+        act(b("x2", 0, Z), P(7, Z, 2 * Z), F.Abs)
+        act(b("a12", 0, Z), P(7, 0, Z), F.Relu, bias=-128.0 * (C + 63.5), scale=128.0)
+        act(b("a12", Z), b("x2", 0, Z), F.Relu, bias=256.0, scale=-128.0)
+        for j in range(2):
+            act(b("Tw", 384 * j, 384 * j + 384), P(1 + j, 0, 384))
+        choices(t)
+        mm(P(4, 0, Z), mat("Wb", "U"), b("nD", 3 - t, V, 4), True, False)
+        mm(P(5, 0, Z), mat("Wb", "I"), b("a12", 0, Z), True, False)
+        mm(P(5, 0, Z), mat("Wb", "I"), b("a12", Z), False, False)
+        mm(P(3, 0, 12), mat("W32", "I"), b("dum"), True, False)
+        for j in range(2):
+            tt(b("z2", 384 * j, 384 * j + 384), gat(b("Tw"), "asku", 384 * j, 384 * j + 384), b("za", 384 * j, 384 * j + 384), A.mult)
+            for l in range(4):
+                mm(P(4, 96 * j, 96 * j + 96), mat("Wb", "I"), b("z2", 384 * j + l, 384 * j + 384, 4), False, j == 1 and l == 3)
+        act(b("vc"), b("cp"), scale=-1.0)
+        act(b("vs"), ind(b("sigr", Z), b("Yu", 0, 24)))
+        ts(b("nvt"), P(4, 0, Z), col(6), A.is_gt)
+        mm(P(5, 0, Z), b("Bb"), b("nvt"), False, True)
+        ts(b("aw", o, C, 16), P(5, 0, Z), 30.0, A.is_le)
+        act(b("blk", 2 * V + 96), gat(b("aw"), "blu", 2 * V + 96, 2 * V + Z))
+        cp(b("blk", 2 * V, 2 * V + 96), gat(b("aw"), "blu", 2 * V, 2 * V + 96))
+        mm(P(6, 0, Z), mat("Wb", "I"), b("blk", 2 * V), True, False)
+        for j in range(2):
+            act(b("blk", V + 384 * j, V + 384 * j + 384), gat(b("aw"), "blu", V + 384 * j, V + 384 * j + 384))
+            cp(b("blk", 384 * j, 384 * j + 384), gat(b("aw"), "blu", 384 * j, 384 * j + 384))
+            for e in range(2):
+                for k in range(4):
+                    mm(P(6, 96 * j, 96 * j + 96), mat("Wb", "I"), b("blk", V * e + 384 * j + k, V * e + 384 * j + 384, 4), False, j == 1 and e == 1 and k == 3)
+        ts(b("eff", Z), b("aw", o, C, 16), 2.0, A.mult)
+        tt(b("eff", 0, Z), P(6, 0, Z), b("eff", Z), A.is_lt)
+        for i in range(16):
+            mm(P(3, 0, 12), m4("Gb", i), b("eff", i, Z, 16), False, i == 15)
+        act(b("K", 3 - t, V, 4), b("eff", 0, Z), scale=56.0)
+        tt(b("x2", 0, Z), b("x1", 0, Z), b("eff", 0, Z), A.mult)
+        tt(b("S1", Z + 3 - t, None, 4), b("S1", Z + 3 - t, None, 4), b("x2", 0, Z), A.add)
+        act(b("vi"), ind(b("invr", Z), b("Yu", 48, 72)))
+        tt(b("of", 72, 84), P(3, 0, 12), b("Yq", 72, 84), A.min)
+        ts(b("ofu", 72, 84), b("of", 72, 84), 8192.0, A.mult, float(Z), A.add)
+        for j in range(6):
+            act(b("of6", 12 * j, 12 * j + 12), P(3, 0, 12))
+        cp(ind(b("S1"), b("ofu", 72, 84)), b("nS"))
+        if t == 0:
+            act(b("nv"), b("nv"), scale=-2.0 ** -12)
+            act(b("v4"), b("v4"), scale=4.0)
+
+    clear2(2)
+    for j in range(2):
+        act(b("S1", Z + vb[j][0], Z + vb[j][1]), P(4 + j, 0, vb[j][1] - vb[j][0]), F.Relu, scale=-1.0)
+    nb = NB // 16
+    for l in range(4):
+        for r in range(4):
+            mm(P(7, nb * l, nb * l + nb), m4("PL", 4 * l + r), b("fa", r, NB // 4, 4), r == 0, r == 3)
+
+    def masked(win, banks):
+        for (c0, c1, op), p in zip(((NV, V, A.mult), (0, NV, A.min)), banks):
+            for k in range(4):
+                tt(b(win, 4 * c0 + k, 4 * c1, 4), b("c0", 4 * c0 + k, 4 * c1, 4), P(p, 0, c1 - c0), op)
+    masked("wa", (2, 3))
+    ts(b("plu"), P(7, 0, 4 * nb), -63.75, A.add)
+    act(b("df"), b("s32a"), F.Relu, scale=-2.0 ** 26)
+
+    def sweep32(win, kind):
+        mm(P(5, 0, V - NB), mat("W32", kind), b("v4", NB), True, False)
+        for l in range(4):
+            tt(b("acc", NB * (l % 2), NB * (l % 2) + NB), gat(b(win), "plu", NB * l, NB * l + NB),
+               b("v4", 0, NB) if l == 0 else b("acc", NB - NB * (l % 2), 2 * NB - NB * (l % 2)), A.add)
+        for c0, c1 in ((0, 256), (256, 576), (576, 960), (960, 1408)):
+            act(b("z32", c0, c1), gat(b(win), "invu", 4 * NB + c0, 4 * NB + c1))
+            for k in range(4):
+                mm(P(5, c0 // 4, c1 // 4), mat("W32", kind), b("z32", c0 + k, c1, 4), False, c1 == 1408 and k == 3)
+    ts(b("wa", C, C + 448), b("wa", C, C + 448), -4096.0, A.mult, 0.0, A.max)
+    act(b("wa", C + 448), b("wa", C + 448), F.Relu, scale=-4096.0)
+    sweep32("wa", "D")
+    mm(P(4, 0, NB), mat("W32", "D"), b("acc", NB), True, True)
+    act(b("t32", NB), P(5, 0, V - NB), scale=0.25)
+    ts(b("t32", 0, NB), P(4, 0, NB), 0.25, A.mult)
+    exchange(-1, "s32b", "wb", C, lambda c0, c1: tt(b("s32b", c0, c1), gat(b("t32"), "bsl", c0, c1), b("df", c0, c1), A.min))
+    for j, (c0, c1) in enumerate(((NV, V), (0, NV))):
+        mm(P(j, 0, c1 - c0), mat("W32", "U"), b("t32", c0, c1), True, True)
+    masked("wb", (0, 1))
+    act(b("Ts"), b("S1", Z), F.Sign, bias=-1.0 / 32)
+    for j in range(2):
+        mm(P(6 + j, 0, 384), mat("Wb", "U"), b("Ts", 384 * j, 384 * j + 384), True, True)
+        act(b("K", 384 * j, 384 * j + 384), P(6 + j, 0, 384), bias=0.125, scale=0.125)
+    for j in range(2):
+        mm(P(2 + j, 0, 384), mat("Wh", "I"), b("Lqc", 384 * j, 384 * j + 384), True, False)
+        mm(P(2 + j, 0, 384), b("Un32"), b("S1", Z + 384 * j, Z + 384 * j + 384), False, True)
+        act(b("nH", 384 * j, 384 * j + 384), P(2 + j, 0, 384), bias=512.0)
+    for tok in ends:
+        wait("g", tok)
+    wait("y", landed[0])
+    dma("y", [(T.pay[:], b("nH"))])
+    sweep32("wb", "I")
+    tt(b("nv", 0, NB), b("acc", NB), b("K", 0, NB), A.mult)
+    dma("y", [(T.mu[:, 0:NB], b("nv", 0, NB))])
+    tt(b("nv", NB), P(5, 0, V - NB), b("K", NB), A.mult)
+    dma("s", [(T.mu[:, NB:V], b("nv", NB))])
+    for tok in ends:
+        wait("g", tok)
+    for s, n in cnt.items():
+        wait("g", (s, n))

@@ -6,8 +6,14 @@ C = 4 * V
 E = (NR - 1) * X
 Z = 192
 NV = 512
-SV = 768
-NB = 416
+SV = 1024
+NS = C + E - SV
+NB = 448
+LEAD = {1:(4,),-1:(2,)}
+NH = 256
+QT = 1
+CW = 512
+QAT = 2
 f32, bf, i32, u16, f16 = "float32", "bfloat16", "int32", "uint16", "float16"
 
 
@@ -20,25 +26,26 @@ SCRATCH = {
     "io": sb(512, f32), "W32": sb(256, f32), "Wb": sb(256, bf), "Wh": sb(256, f16), "Wq": sb(256, f16), "Un": sb(128, bf), "Gb": sb(2048, bf),
     "Fm": sb(512, bf), "Am": sb(512, f32), "Bm": sb(512, f32), "Em": sb(512, f32), "Rm": sb(128, f32), "B32": sb(128, f32), "Bb": sb(128, bf),
     "one": sb(128, f32), "pi": sb(8, i32), "pp": sb(16, f32), "kq": sb(Z, f32), "cX": sb(NV, bf), "dum": sb(12, f32),
-    "c5": sb(384, bf), "Wq32": sb(128, f32), "Dn": sb(128, f16), "Un32": sb(128, f32), "of6": sb(72, f32), "Yq": sb(84, f32),
-    "sigr": sb(Z + C, f32), "invr": sb(Z + C + E, f32), "Cx": sb(Z + C + E, bf), "S1": sb(Z + V, f32),
+    "Wq32": sb(128, f32), "ch": sb(V, f16), "Un32": sb(128, f32), "Yq": sb(84, f32),
+    "clm": sb(C, f32), "lwr": sb(V, f16), "invr": sb(Z + C + E, f32), "Cx": sb(Z + C + E, bf), "S1": sb(Z + V, f32),
     "Dw": sb(C + E, f32), "Lq": sb(V + E, f32), "Lqc": sb(V, f16), "p1h": sb(V, f16), "nH": sb(V, f32), "K": sb(V, bf),
-    "rh": sb(C, f16), "r32": sb(C - 4 * NV, f32), "nD": sb(V, bf), "df": sb(E, bf), "z32": sb(C + E - SV, f32), "zb": sb(C, bf),
+    "rh": sb(C, f16), "r32": sb(C - 4 * NV, f32), "nD": sb(V, bf), "df": sb(E, bf), "z32": sb(Z + C, f32), "zb": sb(C, bf),
     "c0": sb(C + E, bf), "Tw": sb(V + E, bf), "Ts": sb(V, bf), "t32": sb(V, f32), "wa": sb(C + E, f32), "wb": sb(C + E, f32),
-    "za": sb(V, bf), "z2": sb(V, bf), "nvt": sb(Z, bf), "a12": sb(2 * Z, bf), "aw": sb(C, bf), "blk": sb(2 * V + Z, bf), "eff": sb(2 * Z, bf),
-    "sA": sb(E, f16), "sB": sb(E, f16), "sC": sb(E, bf), "sD": sb(E, bf), "lA": sb(E, f16), "lB0": sb(E, f16), "lB1": sb(E, f16),
+    "za": sb(V, bf), "z2": sb(V, bf), "nvt": sb(Z, bf), "a12": sb(2 * Z, bf), "aw": sb(C, bf), "blk": sb(2 * V, bf), "eff": sb(Z, bf),
+    "sA": sb(E, f16), "sB": sb(E, f16), "sC": sb(E, bf), "sD": sb(E, bf), "lA": sb(E, f16), "lB": sb(E, f16),
     "ia": sb(248, i32), "ib": sb(248, i32), "ic": sb(248, i32), "fa": sb(248, f32), "fb": sb(248, f32), "fc": sb(Z, f32),
     "qu": sb(248, u16), "xbu": sb(56, u16), "atu": sb(Z, u16), "sigu": sb(Z, u16), "invu": sb(248, u16), "bsl": sb(56, u16), "plu": sb(NB // 4, u16),
-    "mk": sb(Z, f32), "asku": sb(48, u16), "qbu": sb(48, u16), "lvu": sb(48, u16), "blu": sb(108, u16), "L96": sb(108, f32), "lw": sb(48, i32),
-    "X0": sb(144, f32), "X1": sb(240, f32), "thr": sb(60, f32), "km": sb(48, f32), "Y": sb(120, f32), "Yu": sb(120, u16),
+    "mk": sb(96, f32), "asku": sb(48, u16), "qbu": sb(48, u16), "lvu": sb(48, u16), "blu": sb(96, u16), "L96": sb(96, f32), "lw": sb(48, i32),
+    "X0": sb(144, f32), "X1": sb(240, f32), "thr": sb(96, f32), "km": sb(48, f32), "Y": sb(120, f32), "Yu": sb(120, u16), "sw": sb(96, f32),
     "of": sb(84, f32), "ofu": sb(84, u16), "vs": sb(2 * Z, f32), "vi": sb(2 * Z, f32), "vc": sb(2 * Z, bf), "cp": sb(2 * Z, f32),
     "x1": sb(2 * Z, f32), "x2": sb(2 * Z, f32), "nS": sb(Z, f32),
 }
 for _b in range(8):
     SCRATCH["P%d" % _b] = ("psum", [128, 512], f32)
-ALIAS = {"lwr": ("z32", V), "msg": ("blk", V), "G32": ("wa", 2048), "PL": ("wb", 2048), "s32a": ("Lq", E), "s32b": ("Dw", E), "acc": ("r32", 2 * NB)}
+ALIAS = {"sigr": ("z32", Z + C), "msg": ("blk", V), "PL": ("wb", 2048), "s32a": ("Lq", E), "s32b": ("Dw", E), "acc": ("r32", 2 * NB)}
 NX = 10
-SEMAPHORES = ["qv", "qs", "qt", "qg"] + ["ar%d" % x for x in range(NX)] + ["ls%d" % x for x in range(NX)] + ["d%d" % x for x in range(30)]
+SEMAPHORES = (["qv", "qs", "qt", "qg"] + ["ar%d" % x for x in range(NX)] + ["br%d" % x for x in range(NX)] + ["ls%d" % x for x in range(NX)]
+              + ["d%d" % x for x in range(30)])
 
 
 def b(name, c0=0, c1=None, st=1, p=None):
@@ -49,6 +56,10 @@ def b(name, c0=0, c1=None, st=1, p=None):
 
 def ind(win, off):
     return win[:5] + (off,)
+
+
+def pieces(*cuts):
+    return list(zip(cuts, cuts[1:]))
 
 
 def rank_program(g, core, T, topo):
@@ -133,10 +144,10 @@ def rank_program(g, core, T, topo):
     def act(o, i, fn=F.Identity, bias=None, scale=None):
         kw = {}
         if bias is not None:
-            kw["bias"] = bias
+            kw["bias"] = ap(bias)
         if scale is not None:
             kw["scale"] = scale
-        emit("s", lambda: g.scalar.activation(ap(o), ap(i), fn, **kw), o, [i])
+        emit("s", lambda: g.scalar.activation(ap(o), ap(i), fn, **kw), o, [i, bias])
 
     def mm(o, l, r, start, stop):
         emit("t", lambda: g.tensor.matmul(ap(o), ap(l), ap(r), start, stop), o, [l, r])
@@ -166,9 +177,9 @@ def rank_program(g, core, T, topo):
         c = T.cores[r]
         dst = [(r + sign * (j + 1)) % NR for j in range(NR - 1)]
         near = [j for j in range(NR - 1) if topo.chip(T.cores[dst[j]]) == topo.chip(c)]
-        first = list(range(4)) if min(near) >= 4 else list(range(3, 7))
         calls = []
-        for part in (first, [j for j in range(NR - 1) if j not in first]):
+        lead = [EARLY[i:j] for i, j in pieces(0, *LEAD[sign])]
+        for part in lead + [[j for j in range(NR - 1) if j not in sum(lead, [])]]:
             far = [j for j in part if j not in near]
             en = topo.engines(c, T.cores[dst[far[0]]])
             w = len(en) // len(far)
@@ -176,33 +187,44 @@ def rank_program(g, core, T, topo):
             for j in part:
                 if j in near:
                     row.append((j, dst[j], sum(1 << e for e in topo.engines(c, T.cores[dst[j]]) if e not in en)))
-            calls.append((min(part) * X, (max(part) + 1) * X, row))
+            calls.append(row)
         return calls
 
+    EARLY = [j for j in range(NR - 1) if all(topo.chip(T.cores[(r + s * (j + 1)) % NR]) != topo.chip(T.cores[r]) for r in range(NR) for s in (1, -1))][:4]
+    E0, E1 = EARLY[0] * X, (EARLY[-1] + 1) * X
+    LATE = [(E1, E), (0, E0)]
     nx = [0]
     landed = [None]
 
-    def exchange(sign, src, land, l0, make):
+    def exchange(sign, src, land, l0, make, between=None):
         x = nx[0]
         nx[0] += 1
         sent = 0
-        for c0, c1, row in plan(rank, sign):
-            make(c0, c1)
-            deps("g", None, [b(src, c0, c1)], [])
+        cuts = [E0 + X * i for i in (0,) + LEAD[sign]]
+        for n, row in enumerate(plan(rank, sign)):
+            last = n == len(LEAD[sign])
+            cols = [(cuts[-1], E), (0, E0)] if last else [pieces(*cuts)[n]]
+            sem = "ab"[last] + "r%d" % x
+            if last and between:
+                between()
+            for c0, c1 in cols:
+                make(c0, c1)
+            deps("g", None, [b(src, c0, c1) for c0, c1 in cols], [])
             trs = []
             for j, d, m in row:
                 rid, pid, _ = topo.addr(T.cores[d])
-                trs.append(RemoteDMATransfer(dst_ids=[DstId(rid=rid, pnc=pid)], dma_engine_mask=m, remote_sem=T.sem["ar%d" % x],
+                trs.append(RemoteDMATransfer(dst_ids=[DstId(rid=rid, pnc=pid)], dma_engine_mask=m, remote_sem=T.sem[sem],
                                              src=ap(b(src, j * X, (j + 1) * X)), dst=T[land][:, l0 + j * X:l0 + (j + 1) * X]))
                 sent += bin(m).count("1")
             g.remote_dma_fused(trs, local_sem=T.sem["ls%d" % x])
+            tok = (sem, sum(bin(m).count("1") for r in range(NR) if r != rank
+                            for call in (plan(r, sign)[-1:] if last else plan(r, sign)[:-1]) for j, d, m in call if d == rank))
+            clock[tok] = {}
+            landed[0] = tok
+            for c0, c1 in cols:
+                hist.setdefault(land, []).append((l0 + c0, l0 + c1, 1, True, None, tok))
         note("g", None, [b(src)], [], ("ls%d" % x, sent))
         ends.append(("ls%d" % x, sent))
-        got = sum(bin(m).count("1") for r in range(NR) if r != rank for _, _, row in plan(r, sign) for j, d, m in row if d == rank)
-        tok = ("ar%d" % x, got)
-        clock[tok] = {}
-        landed[0] = tok
-        hist.setdefault(land, []).append((l0, l0 + E, 1, True, None, tok))
 
     def mat(name, kind):
         c = {"I": 0, "D": 16, "U": 112}[kind]
@@ -220,14 +242,12 @@ def rank_program(g, core, T, topo):
     def gat(win, lst, c0, c1):
         return ind(win, b(lst, c0 // 16, c1 // 16))
 
-    ROW = (0, 128, 18)
-    halves = ((0, 448), (448, 896))
+    ROW, ROW2 = (0, 128, 18), (14, 113, 14)
     vb = ((0, NV), (NV, V))
-    GP = [[256, 16], [-16, 8], [-257, 16]]
+    GP = [[256, 16], [-ROW[2], 8], [-256, 16]]
 
     def spread(dst, src):
-        wait("y", landed[0])
-        dma("y", [(b(dst, Z, None, 1, (i, 128, 16)), src) for i in range(16)])
+        dma("y", [(b(dst, Z, None, 1, ROW), src)])
 
     def round_matrices(t):
         o = 4 * (3 - t)
@@ -238,24 +258,20 @@ def rank_program(g, core, T, topo):
 
     dma("y", [(b("xs", Z, 248), T.xpt[:])])
     dma("s", [(b("dbt"), T.debt[:])])
-    dma("y", [(b("xs", 0, Z), T.sig[:])])
-    dma("s", [(b("csh"), T.cash[:])])
-    dma("y", [(b("col"), T.coll[:])])
     iota(b("pi", 0, 1), [[0, 1]], 0, 1)
     iota(b("io"), [[1, 512]], 0, 0)
-    ms(b("W32"), 1.0)
     ms(b("fb"), 0.0)
+    dma("y", [(b("wb", 0, None, 1, ROW2), b("fb"))])
+    dma("y", [(b("xs", 0, Z), T.sig[:])])
+    dma("y", [(b("invr", Z, None, 1, ROW), b("fb"))])
+    dma("y", [(b("col"), T.coll[:])])
+    dma("y", [(b("csh"), T.cash[:]), (b("thi", 0, 1), T.th[:])])
+    for c0 in range(0, V, Z):
+        act(b("K", c0, c0 + Z), b("fb", 0, Z), F.Silu)
+    ms(b("W32"), 1.0)
     ms(b("one"), 1.0)
     ms(b("B32"), 4.0)
     asel(b("W32"), b("W32"), [[0, 2], [-1, 128]], 0, 1)
-    dma("y", [(b("invr", Z, None, 1, ROW), b("fb")), (b("wb", 0, None, 1, ROW), b("fb"))])
-    dma("y", [(b("thi", 0, 1), T.th[:])])
-    NS = C + E - SV
-    iota(b("z32", NS - 1024, NS), [[1, 1024]], 64 + C + E - 1024, 0)
-    for c0 in range(0, NS - 1024, 512):
-        n = min(512, NS - 1024 - c0)
-        act(b("z32", c0, c0 + n), b("io", 0, n), bias=float(64 + SV + c0))
-    act(b("Wb"), b("W32"))
     p0 = b("pi", 0, 1)
     ts(b("pi", 1, 2), p0, 3, A.bitwise_and)
     ts(b("pi", 2, 3), p0, 2, A.arith_shift_right, 3, A.bitwise_and)
@@ -266,19 +282,27 @@ def rank_program(g, core, T, topo):
     ts(col(5), col(3), -float(Z), A.add, 1.0 / 8192, A.mult)
     ts(col(4), col(1), 192.0, A.mult)
     ts(col(8), col(1), 192.0, A.mult, col(2), A.add)
+    for t in range(2):
+        ts(col(11 + t), col(8), 768.0 * (3 - t), A.add)
+    for c0, c1 in pieces(NS - E, NS - E + 512, NS):
+        act(b("z32", c0, c1), b("io", 0, c1 - c0), bias=float(64 + SV + c0))
+    iota(b("z32", 1024, NS - E), [[1, NS - E - 1024]], 64 + SV + 1024, 0)
+    for c0, c1 in pieces(0, 512, 1024):
+        ts(b("z32", c0, c1), b("io"), float(64 + SV + c0), A.add)
     ts(b("ic", Z, 248), b("xs", Z, 248), 2, A.arith_shift_right)
     cp(b("xbu"), b("ic", Z, 248))
-    ts(b("ia"), b("xs"), 4, A.arith_shift_right)
-    ts(b("ib"), b("xs"), 248.0, A.mult)
-    ts(b("ia"), b("ia"), -3967.0, A.mult)
-    tt(b("ia"), b("ia"), b("ib"), A.add)
-    cp(b("qu"), b("ia"))
-    act(ind(b("wb"), b("qu", SV // 16, 248)), b("z32", 0, NS), F.Silu)
-    act(b("Un"), mat("W32", "U"), scale=-1.0)
-    act(b("Un32"), mat("W32", "U"), scale=-1.0)
-    act(b("Wq32"), mat("W32", "I"), scale=0.25)
-    exchange(1, "sA", "lA", 0, lambda c0, c1: ts(b("sA", c0, c1), gat(b("dbt"), "xbu", c0, c1), -512.0, A.add))
-    iota(b("c5"), [[0, 384]], -512, 0)
+
+    def places(c0, c1):
+        ts(b("ia", c0, c1), b("xs", c0, c1), 4, A.arith_shift_right)
+        ts(b("ib", c0, c1), b("xs", c0, c1), 248.0, A.mult)
+        ts(b("ia", c0, c1), b("ia", c0, c1), -3967.0, A.mult)
+        tt(b("ia", c0, c1), b("ia", c0, c1), b("ib", c0, c1), A.add)
+        cp(b("qu", c0, c1), b("ia", c0, c1))
+    exchange(1, "sA", "lA", 0, lambda c0, c1: ts(b("sA", c0, c1), gat(b("dbt"), "xbu", c0, c1), -512.0, A.add), lambda: places(Z, 248))
+    act(ind(b("wb"), b("qu", Z, 248)), b("z32", NS - E, NS), F.Silu)
+    places(SV // 16, Z)
+    act(ind(b("wb"), b("qu", SV // 16, Z)), b("z32", 0, NS - E), F.Silu)
+    iota(b("cX"), [[0, NV]], -128, 0)
     asel(b("B32"), b("B32"), [[-16, 8], [0, 16]], 0, 1, A.is_ge)
     asel(b("B32"), b("B32"), [[16, 8], [0, 16]], 15, -1, A.is_ge)
     for h in range(4):
@@ -287,52 +311,57 @@ def rank_program(g, core, T, topo):
     asel(b("Rm"), b("Rm"), [[16, 8], [0, 4], [4, 4]], 3, -1, A.is_ge)
     for h in range(4):
         asel(m4("Em", h), b("Rm"), [[0, 8], [1, 4], [0, 4]], -h, 0)
-    iota(b("K"), [[0, V]], 0, 0)
-    iota(b("cX"), [[0, NV]], -128, 0)
     iota(b("kq"), [[1, 4], [0, 48]], 0, 0)
     round_matrices(0)
-    wait("y", landed[0])
-    dma("y", [(b("v4"), T.val[:]), (b("nv", 0, None, 1, (0, 112)), T.val[16:128, :]), (b("nv", 0, None, 1, (112, 128)), T.val[0:16, :])])
+    iota(b("z32", NS), [[0, Z + C - NS]], 0, 0)
+    act(b("Un32"), mat("W32", "U"), scale=-1.0)
+    act(b("Wq32"), mat("W32", "I"), scale=0.25)
+    cp(b("Wh"), b("W32"))
+    cp(b("Wb"), b("W32"))
     ts(b("Wq"), b("W32"), 0.25, A.mult)
+    ts(b("Un"), mat("W32", "U"), -1.0, A.mult)
+    places(0, SV // 16)
     ts(b("ic", 0, Z), b("xs", 0, Z), 2, A.arith_shift_right)
     ts(b("ib", 0, Z), b("xs", 0, Z), -2304.0, A.add)
-    cp(b("t32"), b("csh"))
+    ts(b("ch"), b("csh"), -512.0, A.add)
     tt(b("ib", 0, Z), b("ib", 0, Z), b("ic", 0, Z), A.max)
     ts(b("Lq", 0, V), b("dbt"), 0.25, A.mult)
     cp(b("atu"), b("ib", 0, Z))
-    cp(b("Wh"), b("W32"))
     for c0 in range(0, SV, 512):
         n = min(512, SV - c0)
         ts(gat(b("invr", Z), "qu", c0, c0 + n), b("io", 0, n), 1.0, A.mult, float(64 + c0), A.add)
     dma("y", [(b("fa"), b("invr", Z, None, 1, ROW))])
-    dma("y", [(b("fb"), b("wb", 0, None, 1, ROW))])
+    dma("y", [(b("fb"), b("wb", 0, None, 1, ROW2))])
+    dma("y", [(b("v4"), T.val[:]), (b("nv", 0, None, 1, (0, 112)), T.val[16:128, :]), (b("nv", 0, None, 1, (112, 128)), T.val[0:16, :])])
+    dma("y", [(b("aw", c0, c0 + V), b("K")) for c0 in range(0, C, V)])
 
     for j in range(2):
-        mm(P(4 + j, 0, 384), mat("W32", "I"), b("t32", 384 * j, 384 * j + 384), True, False)
-        mm(P(4 + j, 0, 384), mat("Wb", "I"), b("c5"), False, False)
-    for j, (c0, c1) in enumerate(vb):
-        mm(P(6 + j, 0, c1 - c0), mat("W32", "I"), b("t32", c0, c1), True, False)
+        mm(P(4 + j, 0, 384), mat("Wh", "I"), b("ch", 384 * j, 384 * j + 384), True, False)
+    for i, (a0, a1) in enumerate(vb):
+        mm(P(6 + i, 0, a1 - a0), mat("Wh", "I"), b("ch", a0, a1), True, False)
         for k in range(4):
-            mm(P(6 + j, 0, c1 - c0), mat("Wb", "I"), b("col", 4 * c0 + k, 4 * c1, 4), False, k == 3)
-        act(b("nH", c0, c1), P(6 + j, 0, c1 - c0), bias=0.0 if j == 0 else -512.0)
-    for j, (c0, c1) in enumerate(halves):
-        mm(P(j, 0, 448), mat("Wq", "U"), b("lA", c0, c1), True, True)
-        ts(b("Lq", V + c0, V + c1), P(j, 0, 448), 128.0, A.add)
-    for j in range(4):
-        tt(b("rh", 768 * j, 768 * j + 768), gat(b("Lq"), "atu", 768 * j, 768 * j + 768), b("col", 768 * j, 768 * j + 768), A.max)
+            if i == 0:
+                mm(P(6, 0, NV), b("Un"), b("cX"), False, False)
+            mm(P(6 + i, 0, a1 - a0), mat("Wb", "I"), b("col", 4 * a0 + k, 4 * a1, 4), False, k == 3)
+    for k, (c0, c1) in enumerate([(E0, E1)] + LATE):
+        mm(P(k, 0, c1 - c0), mat("Wq", "U"), b("lA", c0, c1), True, True)
+        ts(b("Lq", V + c0, V + c1), P(k, 0, c1 - c0), 128.0, A.add)
+    for j, (c0, c1) in enumerate(pieces(0, 768, 1536, 2560, C)):
+        tt(b("rh", c0, c1), gat(b("Lq"), "atu", c0, c1), b("col", c0, c1), A.max)
         for k in range(4):
-            mm(P(4 + j // 2, Z * (j % 2), Z * (j % 2) + Z), mat("Wh", "I"), b("rh", 768 * j + k, 768 * j + 768, 4), False, j % 2 == 1 and k == 3)
-        if j == 2:
+            mm(P(4 + j // 2, c0 // 4 % 384, (c1 // 4 - 1) % 384 + 1), mat("Wh", "I"), b("rh", c0 + k, c1, 4), False, j % 2 == 1 and k == 3)
+        if j == 1:
+            act(b("S1", Z, Z + 384), P(4, 0, 384))
+        if j == QT:
             mm(P(2, 0, 248), mat("W32", "I"), b("fa"), True, False)
-    mm(P(2, 0, 248), mat("W32", "I"), b("fb"), False, True)
-    cp(b("S1", Z, Z + 384), P(4, 0, 384))
+            mm(P(2, 0, 248), mat("W32", "I"), b("fb"), False, True)
+        if j == QAT:
+            ts(b("qu"), P(2, 0, 248), -63.75, A.add, C - 0.75, A.min)
     cp(b("S1", Z + 384), P(5, 0, 384))
-    ts(b("qu"), P(2, 0, 248), -63.75, A.add, C - 0.75, A.min)
 
     def open_sums():
         for j, (c0, c1) in enumerate(vb):
-            mm(P(4 + j, 0, c1 - c0), mat("W32", "D"), b("nH", c0, c1), True, False)
-            mm(P(4 + j, 0, c1 - c0), b("Dn"), b("Lqc", c0, c1), False, False)
+            mm(P(4 + j, 0, c1 - c0), mat("Wh", "D"), b("ch", c0, c1), True, False)
             mm(P(4 + j, 0, c1 - c0), mat("Wb", "D"), b("K", c0, c1), False, False)
 
     def first_lists():
@@ -342,182 +371,223 @@ def rank_program(g, core, T, topo):
         ts(b("Lqc"), b("dbt"), -512.0, A.add)
         for j in range(2):
             tt(b("p1h", 384 * j, 384 * j + 384), P(4 + j, 0, 384), b("Lqc", 384 * j, 384 * j + 384), A.min)
-        ts(b("Dn"), mat("W32", "D"), -1.0, A.mult)
-        ts(b("Cx", Z + C), gat(b("col"), "qu", C, C + E), -1.0, A.mult)
+        for j, (c0, c1) in enumerate(vb):
+            tt(b("ch", c0, c1), P(6 + j, 0, c1 - c0), b("Lqc", c0, c1), A.subtract)
+        if CW:
+            act(b("Cx", Z + C, Z + C + CW), gat(b("col"), "qu", C, C + CW), scale=-1.0)
+        if CW < E:
+            ts(b("Cx", Z + C + CW), gat(b("col"), "qu", C + CW, C + E), -1.0, A.mult)
         ts(b("fc"), b("xs", 0, Z), 64.0, A.add)
-        ts(col(6), b("thi", 0, 1), -1.0, A.mult, 16.0, A.add)
-        ts(b("dum"), b("io", 0, Z, 16), 1.0 / 8192, A.mult, col(5), A.add)
+
+    def swap_lists():
+        for c0 in range(36, 84, 12):
+            tt(b("of", c0, c0 + 12), P(3, 0, 12), b("Yq", c0, c0 + 12), A.min)
+        ts(b("ofu", 36), b("of", 36), 8192.0, A.mult, float(Z), A.add)
 
     def swaps():
-        tt(b("of", 0, 72), b("of6"), b("Yq", 0, 72), A.min)
-        ts(b("ofu", 0, 72), b("of", 0, 72), 8192.0, A.mult, float(Z), A.add)
         for e in range(2):
-            act(ind(b("sigr"), b("ofu", 12 * e, 12 * e + 12)), b("vs", Z - Z * e, 2 * Z - Z * e), F.Silu)
+            act(ind(b("sigr"), b("ofu", 12 + 12 * e, 24 + 12 * e)), b("vs", Z - Z * e, 2 * Z - Z * e), F.Silu)
         dma("y", [(b("fc"), b("sigr", Z, None, 1, ROW))])
         for e in range(2):
-            act(ind(b("invr"), b("ofu", 48 + 12 * e, 60 + 12 * e)), b("vi", Z - Z * e, 2 * Z - Z * e), F.Silu)
+            act(ind(b("invr"), b("ofu", 60 + 12 * e, 72 + 12 * e)), b("vi", Z - Z * e, 2 * Z - Z * e), F.Silu)
         dma("y", [(b("fa"), b("invr", Z, None, 1, ROW))])
-        for e in range(2):
-            cp(ind(b("Cx"), b("ofu", 24 + 12 * e, 36 + 12 * e)), b("vc", Z - Z * e, 2 * Z - Z * e))
-        open_sums()
         for j in range(2):
             mm(P(6 + j, 0, 384), mat("W32", "I"), b("S1", Z + 384 * j, Z + 384 * j + 384), True, True)
             tt(b("p1h", 384 * j, 384 * j + 384), P(6 + j, 0, 384), b("Lqc", 384 * j, 384 * j + 384), A.min)
+        open_sums()
+        for e in range(2):
+            cp(ind(b("Cx"), b("ofu", 36 + 12 * e, 48 + 12 * e)), b("vc", Z - Z * e, 2 * Z - Z * e))
 
     def clear2(t):
         close = t == 2
-        land = "lB%d" % (t % 2)
-        exchange(1, "sB", land, 0, lambda c0, c1: tt(b("sB", c0, c1), gat(b("S1", Z), "xbu", c0, c1), b("sA", c0, c1), A.min))
+        o = 4 * (3 - t)
+        exchange(1, "sB", "lB", 0, lambda c0, c1: tt(b("sB", c0, c1), gat(b("S1", Z), "xbu", c0, c1), b("sA", c0, c1), A.min), swap_lists if t else None)
         if t == 0:
-            iota(b("G32"), [[0, 2048]], 1, 0)
-            asel(b("G32"), b("G32"), GP, 0, 1)
+            iota(b("Gb"), [[0, 2048]], 1, 0)
+            asel(b("Gb"), b("Gb"), GP, 0, 1)
             first_lists()
             spread("sigr", b("fc"))
+            spread("invr", b("fa"))
         else:
             swaps()
         if t == 1:
             round_matrices(1)
             iota(b("aw", 12, C, 16), [[0, Z]], 0, 0)
+        (a0, a1), (b0, b1) = LATE
+        wire = [(1, 0, E0, E1, "I", "U"), (2, 0, E0, E1, "D", "I"),
+                (0, 0, a0, a1, "I", "U"), (6, 0, b0, b1, "I", "U"), (3, 0, a0, a1, "D", "I"), (3, a1 - a0, b0, b1, "D", "I")]
+
+        def over(n):
+            k, at, c0, c1, kind, _ = wire[n]
+            mm(P(k, at, at + c1 - c0), mat("Wb", kind), b("Cx", Z + C + c0, Z + C + c1), at == 0, False)
+
+        def paid(n):
+            k, at, c0, c1, _, kind = wire[n]
+            mm(P(k, at, at + c1 - c0), mat("Wq", kind), b("lB", c0, c1), False, n != 4)
+            return P(k, at, at + c1 - c0)
         mm(P(0, 0, 384), mat("Wq", "I"), b("p1h", 0, 384), True, False)
         mm(P(0, 0, 384), b("Un"), b("cX", 0, 384), False, True)
         if t == 0:
             open_sums()
-        for j, (c0, c1) in enumerate(halves):
-            mm(P(2 + j, 0, 448), mat("Wb", "D"), b("Cx", Z + C + c0, Z + C + c1), True, False)
-        mm(P(1, 0, 448), mat("Wb", "I"), b("Cx", Z + C, Z + C + 448), True, False)
-        for l in range(4):
+        for k in (2, 3, 6, 7):
+            mm(P(k, 0, 384), mat("Wq", "I"), b("p1h", 384), True, False)
+        for l, k in enumerate((2, 3, 6, 7)):
             tt(b("Dw", l, 1536, 4), P(0, 0, 384), b("Cx", Z + l, Z + 1536, 4), A.add)
-            mm(P(6 + l % 2, 0, 384), mat("Wq", "I"), b("p1h", 384), True, False)
-            mm(P(6 + l % 2, 0, 384), mat("Wb", "I"), b("Cx", Z + 1536 + l, Z + C, 4), False, True)
-            act(b("Dw", 1536 + l, C, 4), P(6 + l % 2, 0, 384), bias=128.0)
-        mm(P(0, 0, 448), mat("Wb", "I"), b("Cx", Z + C + 448), True, False)
+            mm(P(k, 0, 384), mat("Wb", "I"), b("Cx", Z + 1536 + l, Z + C, 4), False, True)
+            act(b("Dw", 1536 + l, C, 4), P(k, 0, 384), bias=128.0)
+        for n in (0, 1, 4, 5):
+            over(n)
+        ts(b("Dw", C + E0, C + E1), paid(0), 128.0, A.add)
+        over(3)
+        over(2)
+        paid(1)
         ts(b("sigu"), b("fc"), -63.75, A.add)
-        for j, (c0, c1) in enumerate(halves):
-            mm(P(1 - j, 0, 448), mat("Wq", "U"), b(land, c0, c1), False, True)
-        ts(b("Dw", C, C + 448), P(1, 0, 448), 128.0, A.add)
-        act(b("Dw", C + 448), P(0, 0, 448), bias=128.0)
-        for j, (c0, c1) in enumerate(halves):
-            mm(P(2 + j, 0, 448), mat("Wq", "I"), b(land, c0, c1), False, True)
-        mm(P(7, 0, 56), mat("W32", "D"), b("fa", Z, 248), True, True)
-        for j in range(2):
-            ts(b("rh", 1024 * j, 1024 * j + 1024), gat(b("Dw"), "sigu", 1024 * j, 1024 * j + 1024), 0.0, A.max, -128.0, A.add)
-        for j in range(4):
-            act(b("r32", 256 * j, 256 * j + 256), gat(b("Dw"), "sigu", 4 * NV + 256 * j, 4 * NV + 256 * j + 256), F.Relu)
+        ts(b("Dw", C + a0, C + a1), paid(2), 128.0, A.add)
+        act(b("Dw", C + b0, C + b1), paid(3), bias=128.0)
+        mine, theirs = pieces(0, 512, 1280, 4 * NV - 256, 4 * NV), pieces(0, 128, 384, 704, C - 4 * NV)
+        for c0, c1 in mine:
+            ts(b("rh", c0, c1), gat(b("Dw"), "sigu", c0, c1), 0.0, A.max, -128.0, A.add)
+        for j, (c0, c1) in enumerate(theirs):
+            act(b("r32", c0, c1), gat(b("Dw"), "sigu", 4 * NV + c0, 4 * NV + c1), F.Relu)
+        for e, j in ((1, 0), (1, 1), (0, 0), (1, 2), (1, 3), (0, 1), (0, 2), (0, 3)):
+            c0, c1 = (mine, theirs)[e][j]
             for k in range(4):
-                mm(P(5, 64 * j, 64 * j + 64), mat("W32", "D"), b("r32", 256 * j + k, 256 * j + 256, 4), False, j == 3 and k == 3)
-            if j % 2:
-                c0 = 1024 * (j // 2)
-                for k in range(4):
-                    mm(P(4, c0 // 4, c0 // 4 + 256), mat("Wh", "D"), b("rh", c0 + k, c0 + 1024, 4), False, j == 3 and k == 3)
+                mm(P(4 + e, c0 // 4, c1 // 4), mat(("Wh", "W32")[e], "D"), b(("rh", "r32")[e], c0 + k, c1, 4), False, j == 3 and k == 3)
+            if (e, j) == (1, 1):
+                mm(P(7, 0, 56), mat("W32", "D"), b("fa", Z, 248), True, True)
+        paid(4)
+        paid(5)
         ts(b("ib", 0, 56), P(7, 0, 56), 0.25, A.mult, -16.375, A.add)
         cp(b("bsl"), b("ib", 0, 56))
-        if not close:
-            o = 4 * (3 - t)
-            ts(b("X0", 0, 48), b("io", 0, Z, 4), col(8), A.add, 192.0 * o, A.add)
-            ts(b("thr", 0, 48), b("io", 0, Z, 4), 16.0, A.mult, col(9 + t), A.add)
-            ts(b("thr", 48, 60), b("dum"), 16.0 * 8192, A.mult, float(C + o + 1), A.add)
+        for k in range(0 if close else 4):
+            ts(b("msg", k, NV, 4), b("rh", o + k, 4 * NV, 16), -128.0, A.is_gt)
         sg = -1.0 if close else 1.0
-        for j, (c0, c1) in enumerate(halves):
-            act(b("df", c0, c1), P(2 + j, 0, 448), bias=128.0 * sg, scale=sg)
+
+        def over_there():
+            for k, at, c0, c1, _, _ in wire[4:]:
+                act(b("df", c0, c1), P(k, at, at + c1 - c0), bias=128.0 * sg, scale=sg)
+        act(b("df", E0, E1), P(2, 0, E1 - E0), bias=128.0 * sg, scale=sg)
         if close:
+            over_there()
             for j in (1, 0):
                 tt(b("t32", *vb[j]), P(4 + j, 0, vb[j][1] - vb[j][0]), b("nv", *vb[j]), A.max)
             exchange(-1, "s32a", "wa", C, lambda c0, c1: tt(b("s32a", c0, c1), gat(b("t32"), "bsl", c0, c1), b("df", c0, c1), A.max))
             for c0, c1, k in ((NV, V, 2), (0, NV, 3)):
                 mm(P(k, 0, c1 - c0), b("Wq32"), b("v4", c0, c1), True, True)
             for j in range(2):
-                act(b("nD", *vb[j]), P(4 + j, 0, vb[j][1] - vb[j][0]), F.Relu, bias=512.0, scale=16384.0)
+                act(b("nD", *vb[j]), P(4 + j, 0, vb[j][1] - vb[j][0]), F.Relu, bias=4096.0, scale=131072.0)
         else:
             act(b("nD", NV), P(5, 0, V - NV), F.Relu, bias=512.0, scale=16384.0)
             ts(b("nD", 0, NV), P(4, 0, NV), 0.0, A.is_ge, 512.0, A.mult)
+            over_there()
             exchange(-1, "sC", "c0", C, lambda c0, c1: tt(b("sC", c0, c1), gat(b("nD"), "bsl", c0, c1), b("df", c0, c1), A.is_lt))
         if t == 0:
-            iota(b("aw"), [[0, C]], 0, 0)
-            spread("invr", b("fa"))
+            ts(col(6), b("thi", 0, 1), -1.0, A.mult, 16.0, A.add)
+            ts(b("dum"), b("io", 0, Z, 16), 1.0 / 8192, A.mult, col(5), A.add)
+            iota(b("clm"), [[1, 16], [16, Z]], 64, 0)
         if t == 1:
             for l in range(4):
                 for r in range(4):
                     asel(m4("PL", 4 * l + r), b("one"), [[-16, 8], [256, 4], [-4, 4]], -l - 256 * r, 1)
         if not close:
             wiring_sums(t)
-        ns = NV if close else 256
-        mm(P(6, 0, V - ns), mat("Wb", "U"), b("nD", ns), True, close)
-        if not close:
-            mm(P(6, 0, NV - ns), mat("Wb", "I"), b("cX", 0, NV - ns), False, True)
-            wiring(t)
-        for j, c0 in enumerate(range(0, 4 * ns, 512)):
-            mm(P(j % 2), mat("Wh", "I"), b("rh", c0, c0 + 512), True, False)
+        mm(P(6, 0, V - NV), mat("Wb", "U"), b("nD", NV), True, True)
+        for j, (c0, c1) in enumerate(pieces(0, 512, 1024, 1536, 4 * NV)):
+            if j == 2 and not close:
+                wiring(t)
+            mm(P(j % 2, 0, c1 - c0), mat("Wh", "I"), b("rh", c0, c1), True, False)
             for k in range(4):
-                mm(P(j % 2, k, 512, 4), b("Un"), b("nD", c0 // 4, c0 // 4 + 128), False, k == 3)
+                mm(P(j % 2, k, c1 - c0, 4), b("Un"), b("nD", c0 // 4, c1 // 4), False, k == 3)
             if close:
-                act(b("c0", c0, c0 + 512), P(j % 2), F.Relu, bias=128.0 * 8192, scale=8192.0)
+                act(b("c0", c0, c1), P(j % 2, 0, c1 - c0), F.Relu, bias=128.0 * 8192, scale=8192.0)
             else:
-                act(b("c0", c0, c0 + 512), P(j % 2), F.Sign, bias=128.0 - 1.0 / 32)
+                act(b("c0", c0, c1), P(j % 2, 0, c1 - c0), F.Sign, bias=128.0 - 1.0 / 32)
         if not close:
+            barred(t)
             for i in range(16):
-                mm(P(3, 0, 48), m4("G32", i), b("lwr", i, V, 16), i == 0, i == 15)
-        ts(b("invu"), b("fa"), -63.75, A.add)
+                mm(P(3, 0, 48), m4("Gb", i), b("lwr", i, V, 16), i == 0, i == 15)
+        steps = [] if close else least()
         for k in range(4):
-            if not close:
-                tt(b("c0", 4 * ns + k, 4 * NV, 4), b("rh", 4 * ns + k, 4 * NV, 4), P(6, 0, NV - ns), A.is_gt)
-            tt(b("c0", 4 * NV + k, C, 4), b("r32", k, None, 4), P(6, NV - ns, V - ns), A.is_gt)
+            for step in steps[k:k + 1]:
+                step()
+            tt(b("c0", 4 * NV + k, C, 4), b("r32", k, None, 4), P(6, 0, V - NV), A.is_gt)
+        for step in steps[4:5]:
+            step()
+        ts(b("invu"), b("fa"), -63.75, A.add)
 
     def wiring_sums(t):
-        act(b("x1", 0, Z), b("io", 0, Z), bias=-(4 * (3 - t) + 65.5), scale=-16.0)
-        for j, m, src in ((1, "Am", "fc"), (0, "Bm", "fa"), (2, "Am", "fa")):
-            for h in range(4):
-                mm(P(3, 48 * j, 48 * j + 48), m4(m, h), b(src, h, Z, 4), h == 0, h == 3)
+        o = 4 * (3 - t)
+        for h in range(4):
+            mm(P(7, 0, 48), m4("Bm", h), b("fa", h, Z, 4), h == 0, h == 3)
+        for k in range(4):
+            act(b("msg", NV + k, V, 4), b("r32", o + k, None, 16), F.Sign)
+        act(b("x1", 0, Z), b("io", 0, Z), bias=-(o + 65.5), scale=-16.0)
+        act(b("X0", 0, 48), b("io", 0, Z, 4), bias=col(11 + t))
+        act(b("thr", 0, 48), b("io", 0, Z, 4), bias=col(9 + t), scale=16.0)
+        act(b("thr", 48, 96), b("thr", 0, 48), bias=-1.0)
+
+    def barred(t):
+        mm(P(3, 64, 64 + Z), b("Rm"), b("fa", 0, Z), True, True)
+        mm(P(3, 64 + Z, 64 + 2 * Z), b("Rm"), b("fa", 0, Z), True, False)
+        mm(P(3, 64 + Z, 64 + 2 * Z), mat("W32", "I"), b("x1", 0, Z), False, True)
+        act(b("x2", 0, Z), P(3, 64 + Z, 64 + 2 * Z), F.Abs)
+        act(b("a12", 0, Z), P(3, 64, 64 + Z), F.Relu, bias=-128.0 * (C + 63.5), scale=128.0)
+        act(b("a12", Z), b("x2", 0, Z), F.Relu, bias=256.0, scale=-128.0)
 
     def wiring(t):
-        ts(b("lvu"), P(3, 48, 96), -63.75, A.add)
-        act(b("msg"), ind(b("Dw"), b("lvu")), F.Sign, bias=-1.0 / 32)
+        for j, src in enumerate(("fc", "fa")):
+            for h in range(4):
+                mm(P(4, 48 * j, 48 * j + 48), m4("Am", h), b(src, h, Z, 4), h == 0, h == 3)
         mm(P(2, 0, Z), mat("W32", "I"), b("kq"), True, False)
         for k in range(4):
             for h in range(4):
                 mm(P(2, 48 * k, 48 * k + 48), m4("Fm", h), b("msg", 4 * h + k, V, 16), False, k == 3 and h == 3)
-        ts(b("ia", 0, 48), P(3, 0, 48), 0.25, A.mult, -16.375, A.add)
-        ts(b("ia", 48, 96), P(3, 0, 48), 0.0625, A.mult, -4.46875, A.add)
+        ts(b("ia", 0, 48), P(7, 0, 48), 0.25, A.mult, -16.375, A.add)
+        ts(b("ia", 48, 96), P(7, 0, 48), 0.0625, A.mult, -4.46875, A.add)
         ts(b("ib", 0, 48), b("ia", 0, 48), 768.0, A.mult, col(4), A.add)
         ts(b("ib", 48, 96), b("ia", 48, 96), -3071.0, A.mult)
-        cp(b("X1", 192, 240), b("ia", 0, 48))
+        ts(b("X1", 192, 240), b("ia", 0, 48), 4.0, A.mult)
         tt(b("ib", 0, 48), b("ib", 0, 48), b("ib", 48, 96), A.add)
+        ts(b("qbu"), b("ib", 0, 48), float(C - 1), A.min)
         ts(b("X0", 48, 96), b("ib", 0, 48), float(C - 1), A.min)
+        ts(b("lwr"), ind(b("sigr", Z), b("qbu")), -64.0 - 2048, A.add)
+        ts(b("lvu"), P(4, 0, 48), -63.75, A.add)
+        ts(b("ic", 0, 48), P(4, 48, 96), 0.25, A.mult, -16.375, A.add)
+        ts(b("ic", 48, 96), P(4, 48, 96), -2368.0, A.add)
         cp(b("X0", 96, 144), b("lvu"))
-        cp(b("qbu"), b("X0", 48, 96))
-        ts(b("ic", 0, 48), P(3, 96, 144), 0.25, A.mult, -16.375, A.add)
-        ts(b("ic", 48, 96), P(3, 96, 144), -2368.0, A.add)
-        act(b("lwr"), ind(b("sigr", Z), b("qbu")), bias=-64.0)
         tt(b("ic", 0, 48), b("ic", 0, 48), b("ic", 48, 96), A.max)
         cp(b("asku"), b("ic", 0, 48))
 
     def least():
-        cp(b("mk", 0, 96), P(2, 0, 96))
-        tt(b("mk", 0, 96), P(2, 96, Z), b("mk", 0, 96), A.min)
-        tt(b("mk", 0, 48), b("mk", 0, 48), b("mk", 48, 96), A.min)
-        ts(b("ia", 0, 48), b("mk", 0, 48), 64.0, A.add)
-        ts(b("ia", 0, 48), b("ia", 0, 48), 3, A.bitwise_and)
-        ts(b("km"), b("ia", 0, 48), col(1), A.is_equal)
+        return [lambda: cp(b("mk", 0, 96), P(2, 0, 96)),
+                lambda: tt(b("mk", 0, 96), P(2, 96, Z), b("mk", 0, 96), A.min),
+                lambda: tt(b("ia", 0, 48), b("mk", 0, 48), b("mk", 48, 96), A.min),
+                lambda: ts(b("ia", 0, 48), b("ia", 0, 48), 3, A.bitwise_and),
+                lambda: ts(b("km"), b("ia", 0, 48), col(1), A.is_equal)]
 
     def choices(t):
         for j in range(3):
             tt(b("X1", 48 * j, 48 * j + 48), b("X0", 48 * j, 48 * j + 48), b("km"), A.mult)
+        ts(b("lw"), P(3, 0, 48), 2048.0, A.add)
         tt(b("L96", 0, 48), b("X0", 96, 144), b("thr", 0, 48), A.min)
-        cp(b("lw"), P(3, 0, 48))
         tt(b("X1", 144, 192), b("lw"), b("km"), A.mult)
-        tt(b("L96", 48, 96), b("lw"), b("thr", 0, 48), A.min)
         for r in range(4):
             mm(P(0, 0, 60), m4("Em", r), b("X1", r, 240, 4), r == 0, r == 3)
+        tt(b("sw", 0, 48), b("lw"), b("thr", 48, 96), A.is_equal)
+        tt(b("sw", 48, 96), b("X1", 192, 240), b("lw"), A.subtract)
+        tt(b("sw", 0, 48), b("sw", 0, 48), b("sw", 48, 96), A.mult)
+        tt(b("sw", 0, 48), b("sw", 0, 48), b("lw"), A.add)
+        tt(b("L96", 48, 96), b("sw", 0, 48), b("thr", 0, 48), A.min)
         cp(b("Yu", 0, 48), P(0, 0, 48))
         act(b("cp"), ind(b("Cx", Z), b("Yu", 24, 48)), scale=-1.0)
         ts(b("ib", 24, 48), P(0, 24, 48), 0.25, A.mult, -0.375, A.add)
         ts(b("ic", 24, 48), P(0, 24, 48), -2304.0, A.add)
         ts(b("ib", 0, 24), P(0, 24, 48), 0.0625, A.mult, -0.46875, A.add)
         ts(b("ic", 0, 24), P(0, 24, 48), 248.0, A.mult)
-        ts(b("Y", 72, 84), P(0, 48, 60), 0.25, A.mult, float(V - 1), A.min)
+        ts(b("Y", 72, 84), P(0, 48, 60), 0.0625, A.mult, float(V - 1), A.min)
         tt(b("Y", 84, 108), b("ib", 24, 48), b("ic", 24, 48), A.max)
         ts(b("ib", 0, 24), b("ib", 0, 24), -3967.0, A.mult)
         tt(b("Y", 108, 120), b("ib", 24, 36), b("ic", 24, 36), A.max)
-        tt(b("L96", 96, 108), P(0, 48, 60), b("thr", 48, 60), A.min)
         tt(b("Y", 48, 72), b("ib", 0, 24), b("ic", 0, 24), A.add)
         cp(b("blu"), b("L96"))
         cp(b("Yu", 48), b("Y", 48))
@@ -527,91 +597,80 @@ def rank_program(g, core, T, topo):
         tt(b("nS"), ind(b("S1", Z), b("Yu", 72, 84)), b("x1", Z), A.add)
         for l in range(4):
             act(b("za", l, V, 4), b("zb", 4 * (3 - t) + l, C, 16))
-        act(b("Yq", 0, 48), P(0, 0, 48), scale=1.0 / 8192)
-        act(b("Yq", 48), b("Y", 48, 84), scale=1.0 / 8192)
-        act(b("x1", 0, Z), b("x1", 0, Z), bias=56.0)
+        act(b("Yq", 12, 60), P(0, 0, 48), scale=1.0 / 8192)
+        act(b("Yq", 60), b("Y", 48, 72), scale=1.0 / 8192)
+        act(b("Yq", 0, 12), b("Y", 72, 84), scale=1.0 / 8192)
+        act(b("vc"), b("cp"), scale=-1.0)
+        act(P(1, 0, Z), b("x1", 0, Z), bias=56.0)
 
     for t in range(2):
         o = 4 * (3 - t)
         clear2(t)
-        least()
-        for j in range(2):
+        bank = ((4, 6), (5, 0))
+        for j, (c0, c1) in enumerate(pieces(0, 512, 1024, 1280, 1536)):
+            ts(b("zb", c0, c1), gat(b("c0"), "invu", c0, c1), 0.0, A.max)
+            act(b("zb", 1536 + c0, 1536 + c1), gat(b("c0"), "invu", 1536 + c0, 1536 + c1), F.Relu)
             for e in range(2):
-                c0 = 1536 * e + 768 * j
-                if e:
-                    act(b("zb", c0, c0 + 768), gat(b("c0"), "invu", c0, c0 + 768), F.Relu)
-                else:
-                    ts(b("zb", c0, c0 + 768), gat(b("c0"), "invu", c0, c0 + 768), 0.0, A.max)
                 for k in range(4):
-                    mm(P(4 + e, Z * j, Z * j + Z), mat("Wb", "D"), b("zb", c0 + k, c0 + 768, 4), k == 0, k == 3)
-        mm(P(7, 0, Z), b("Rm"), b("fa", 0, Z), True, True)
-        mm(P(7, Z, 2 * Z), b("Rm"), b("fa", 0, Z), True, False)
-        mm(P(7, Z, 2 * Z), mat("W32", "I"), b("x1", 0, Z), False, True)
-        ts(b("Ts", 0, 384), P(4, 0, 384), -1.0, A.mult, -4.0, A.add)
-        act(b("Ts", 384), P(5, 0, 384), bias=-4.0, scale=-1.0)
+                    mm(P(bank[e][j // 3], c0 // 4, c1 // 4), mat("Wb", "D"), b("zb", 1536 * e + c0 + k, 1536 * e + c1, 4), k == 0, k == 3)
+        for j, (c0, c1) in enumerate(pieces(0, 320, 384)):
+            ts(b("Ts", c0, c1), P(bank[0][j], c0, c1), -1.0, A.mult, -4.0, A.add)
+            act(b("Ts", 384 + c0, 384 + c1), P(bank[1][j], c0, c1), bias=-4.0, scale=-1.0)
 
         def make_d(c0, c1):
-            m = (c0 + c1) // 2
-            act(b("sD", m, c1), gat(b("Ts"), "bsl", m, c1))
+            m = c1 if c0 == 0 else (c0 + c1 - (E0 if c1 == E else 0)) // 2
+            if m < c1:
+                act(b("sD", m, c1), gat(b("Ts"), "bsl", m, c1))
             cp(b("sD", c0, m), gat(b("Ts"), "bsl", c0, m))
         exchange(-1, "sD", "Tw", V, make_d)
         if t == 0:
-            asel(b("Gb"), b("G32"), GP, 0, 1)
             act(b("Bb"), b("B32"))
         for j in range(2):
             mm(P(1 + j, 0, 384), mat("Wb", "U"), b("Ts", 384 * j, 384 * j + 384), True, True)
-        act(b("x2", 0, Z), P(7, Z, 2 * Z), F.Abs)
-        act(b("a12", 0, Z), P(7, 0, Z), F.Relu, bias=-128.0 * (C + 63.5), scale=128.0)
-        act(b("a12", Z), b("x2", 0, Z), F.Relu, bias=256.0, scale=-128.0)
-        for j in range(2):
             act(b("Tw", 384 * j, 384 * j + 384), P(1 + j, 0, 384))
         choices(t)
         mm(P(4, 0, Z), mat("Wb", "U"), b("nD", 3 - t, V, 4), True, False)
         mm(P(5, 0, Z), mat("Wb", "I"), b("a12", 0, Z), True, False)
         mm(P(5, 0, Z), mat("Wb", "I"), b("a12", Z), False, False)
         mm(P(3, 0, 12), mat("W32", "I"), b("dum"), True, False)
-        for j in range(2):
-            tt(b("z2", 384 * j, 384 * j + 384), gat(b("Tw"), "asku", 384 * j, 384 * j + 384), b("za", 384 * j, 384 * j + 384), A.mult)
+        cut = pieces(0, 512, V)
+        for j, (c0, c1) in enumerate(cut):
+            tt(b("z2", c0, c1), gat(b("Tw"), "asku", c0, c1), b("za", c0, c1), A.mult)
             for l in range(4):
-                mm(P(4, 96 * j, 96 * j + 96), mat("Wb", "I"), b("z2", 384 * j + l, 384 * j + 384, 4), False, j == 1 and l == 3)
-        act(b("vc"), b("cp"), scale=-1.0)
+                mm(P(4, c0 // 4, c1 // 4), mat("Wb", "I"), b("z2", c0 + l, c1, 4), False, j == 1 and l == 3)
         act(b("vs"), ind(b("sigr", Z), b("Yu", 0, 24)))
+        act(b("vi"), ind(b("clm"), b("Yu", 0, 24)))
+        if t == 0:
+            act(b("nv"), b("nv"), scale=-2.0 ** -12)
+        else:
+            act(b("v4"), b("v4"), scale=4.0)
         ts(b("nvt"), P(4, 0, Z), col(6), A.is_gt)
         mm(P(5, 0, Z), b("Bb"), b("nvt"), False, True)
         ts(b("aw", o, C, 16), P(5, 0, Z), 30.0, A.is_le)
-        act(b("blk", 2 * V + 96), gat(b("aw"), "blu", 2 * V + 96, 2 * V + Z))
-        cp(b("blk", 2 * V, 2 * V + 96), gat(b("aw"), "blu", 2 * V, 2 * V + 96))
-        mm(P(6, 0, Z), mat("Wb", "I"), b("blk", 2 * V), True, False)
-        for j in range(2):
-            act(b("blk", V + 384 * j, V + 384 * j + 384), gat(b("aw"), "blu", V + 384 * j, V + 384 * j + 384))
-            cp(b("blk", 384 * j, 384 * j + 384), gat(b("aw"), "blu", 384 * j, 384 * j + 384))
+        for j, (c0, c1) in enumerate(pieces(0, 256, 512, V)):
+            act(b("blk", V + c0, V + c1), gat(b("aw"), "blu", V + c0, V + c1))
+            cp(b("blk", c0, c1), gat(b("aw"), "blu", c0, c1))
             for e in range(2):
                 for k in range(4):
-                    mm(P(6, 96 * j, 96 * j + 96), mat("Wb", "I"), b("blk", V * e + 384 * j + k, V * e + 384 * j + 384, 4), False, j == 1 and e == 1 and k == 3)
-        ts(b("eff", Z), b("aw", o, C, 16), 2.0, A.mult)
-        tt(b("eff", 0, Z), P(6, 0, Z), b("eff", Z), A.is_lt)
+                    mm(P(6, c0 // 4, c1 // 4), mat("Wb", "I"), b("blk", V * e + c0 + k, V * e + c1, 4), e == 0 and k == 0, e == 1 and k == 3)
+        tt(b("eff"), P(6, 0, Z), b("aw", o, C, 16), A.is_lt)
         for i in range(16):
             mm(P(3, 0, 12), m4("Gb", i), b("eff", i, Z, 16), False, i == 15)
-        act(b("K", 3 - t, V, 4), b("eff", 0, Z), scale=56.0)
-        tt(b("x2", 0, Z), b("x1", 0, Z), b("eff", 0, Z), A.mult)
-        tt(b("S1", Z + 3 - t, None, 4), b("S1", Z + 3 - t, None, 4), b("x2", 0, Z), A.add)
-        act(b("vi"), ind(b("invr", Z), b("Yu", 48, 72)))
-        tt(b("of", 72, 84), P(3, 0, 12), b("Yq", 72, 84), A.min)
-        ts(b("ofu", 72, 84), b("of", 72, 84), 8192.0, A.mult, float(Z), A.add)
-        for j in range(6):
-            act(b("of6", 12 * j, 12 * j + 12), P(3, 0, 12))
-        cp(ind(b("S1"), b("ofu", 72, 84)), b("nS"))
-        if t == 0:
-            act(b("nv"), b("nv"), scale=-2.0 ** -12)
-            act(b("v4"), b("v4"), scale=4.0)
+        act(b("K", 3 - t, V, 4), b("eff"), scale=56.0)
+        tt(P(1, Z, 2 * Z), P(1, 0, Z), b("eff"), A.mult)
+        tt(b("S1", Z + 3 - t, None, 4), P(1, Z, 2 * Z), b("S1", Z + 3 - t, None, 4), A.add)
+        for c0 in range(0, 36, 12):
+            tt(b("of", c0, c0 + 12), P(3, 0, 12), b("Yq", c0, c0 + 12), A.min)
+        ts(b("ofu", 0, 36), b("of", 0, 36), 8192.0, A.mult, float(Z), A.add)
+        cp(ind(b("S1"), b("ofu", 0, 12)), b("nS"))
 
     clear2(2)
-    for j in range(2):
-        act(b("S1", Z + vb[j][0], Z + vb[j][1]), P(4 + j, 0, vb[j][1] - vb[j][0]), F.Relu, scale=-1.0)
     nb = NB // 16
     for l in range(4):
         for r in range(4):
             mm(P(7, nb * l, nb * l + nb), m4("PL", 4 * l + r), b("fa", r, NB // 4, 4), r == 0, r == 3)
+    for j in range(2):
+        act(b("S1", Z + vb[j][0], Z + vb[j][1]), P(4 + j, 0, vb[j][1] - vb[j][0]), F.Relu, scale=-1.0)
 
     def masked(win, banks):
         for (c0, c1, op), p in zip(((NV, V, A.mult), (0, NV, A.min)), banks):
@@ -621,29 +680,39 @@ def rank_program(g, core, T, topo):
     ts(b("plu"), P(7, 0, 4 * nb), -63.75, A.add)
     act(b("df"), b("s32a"), F.Relu, scale=-2.0 ** 26)
 
-    def sweep32(win, kind):
-        mm(P(5, 0, V - NB), mat("W32", kind), b("v4", NB), True, False)
-        for l in range(4):
-            tt(b("acc", NB * (l % 2), NB * (l % 2) + NB), gat(b(win), "plu", NB * l, NB * l + NB),
-               b("v4", 0, NB) if l == 0 else b("acc", NB - NB * (l % 2), 2 * NB - NB * (l % 2)), A.add)
-        for c0, c1 in ((0, 256), (256, 576), (576, 960), (960, 1408)):
+    def sweep32(win, kind, first, done):
+        cut = pieces(0, 128, 448, 896, C - 4 * NB)
+        for c0, c1 in hb:
+            for l in range(4):
+                tt(b("acc", NB * (l % 2) + c0, NB * (l % 2) + c1), gat(b(win), "plu", NB * l + c0, NB * l + c1),
+                   b(first, c0, c1) if l == 0 else b("acc", NB - NB * (l % 2) + c0, NB - NB * (l % 2) + c1), A.add)
+        for j, (c0, c1) in enumerate(cut):
             act(b("z32", c0, c1), gat(b(win), "invu", 4 * NB + c0, 4 * NB + c1))
             for k in range(4):
-                mm(P(5, c0 // 4, c1 // 4), mat("W32", kind), b("z32", c0 + k, c1, 4), False, c1 == 1408 and k == 3)
-    ts(b("wa", C, C + 448), b("wa", C, C + 448), -4096.0, A.mult, 0.0, A.max)
-    act(b("wa", C + 448), b("wa", C + 448), F.Relu, scale=-4096.0)
-    sweep32("wa", "D")
-    mm(P(4, 0, NB), mat("W32", "D"), b("acc", NB), True, True)
+                mm(P(5, c0 // 4, c1 // 4), mat("W32", kind), b("z32", c0 + k, c1, 4), False, j == 3 and k == 3)
+            if j >= 2:
+                done(j - 2, *hb[j - 2])
+    hb = pieces(0, NH, NB)
+    mm(P(5, 0, V - NB), mat("W32", "D"), b("v4", NB), True, False)
+    e1 = E0 + X * LEAD[-1][-1]
+    m = (e1 + E + E0) // 2
+    for c0, c1 in ((E0, e1), (e1, m)):
+        ts(b("wa", C + c0, C + c1), b("wa", C + c0, C + c1), -4096.0, A.mult, 0.0, A.max)
+    for c0, c1 in ((m, E), (0, E0)):
+        if c0 < c1:
+            act(b("wa", C + c0, C + c1), b("wa", C + c0, C + c1), F.Relu, scale=-4096.0)
+    sweep32("wa", "D", "v4", lambda j, c0, c1: mm(P(6 - 2 * j, c0, c1), mat("W32", "D"), b("acc", NB + c0, NB + c1), True, True))
+    act(b("t32", 0, NH), P(6, 0, NH), scale=0.25)
     act(b("t32", NB), P(5, 0, V - NB), scale=0.25)
-    ts(b("t32", 0, NB), P(4, 0, NB), 0.25, A.mult)
+    ts(b("t32", NH, NB), P(4, NH, NB), 0.25, A.mult)
     exchange(-1, "s32b", "wb", C, lambda c0, c1: tt(b("s32b", c0, c1), gat(b("t32"), "bsl", c0, c1), b("df", c0, c1), A.min))
     for j, (c0, c1) in enumerate(((NV, V), (0, NV))):
         mm(P(j, 0, c1 - c0), mat("W32", "U"), b("t32", c0, c1), True, True)
     masked("wb", (0, 1))
-    act(b("Ts"), b("S1", Z), F.Sign, bias=-1.0 / 32)
-    for j in range(2):
-        mm(P(6 + j, 0, 384), mat("Wb", "U"), b("Ts", 384 * j, 384 * j + 384), True, True)
-        act(b("K", 384 * j, 384 * j + 384), P(6 + j, 0, 384), bias=0.125, scale=0.125)
+    for k, (c0, c1) in ((6, (0, NB)), (5, (NB, V))):
+        mm(P(k, 0, c1 - c0), mat("W32", "I"), b("v4", c0, c1), True, False)
+        mm(P(k, 0, c1 - c0), b("Un"), b("nD", c0, c1), False, k == 6)
+    act(b("nv", 0, NB), P(6, 0, NB))
     for j in range(2):
         mm(P(2 + j, 0, 384), mat("Wh", "I"), b("Lqc", 384 * j, 384 * j + 384), True, False)
         mm(P(2 + j, 0, 384), b("Un32"), b("S1", Z + 384 * j, Z + 384 * j + 384), False, True)
@@ -652,11 +721,13 @@ def rank_program(g, core, T, topo):
         wait("g", tok)
     wait("y", landed[0])
     dma("y", [(T.pay[:], b("nH"))])
-    sweep32("wb", "I")
-    tt(b("nv", 0, NB), b("acc", NB), b("K", 0, NB), A.mult)
-    dma("y", [(T.mu[:, 0:NB], b("nv", 0, NB))])
-    tt(b("nv", NB), P(5, 0, V - NB), b("K", NB), A.mult)
-    dma("s", [(T.mu[:, NB:V], b("nv", NB))])
+    sweep32("wb", "I", "nv", lambda j, c0, c1: None)
+    act(b("t32", 0, NH), b("acc", NB, NB + NH), F.Relu, scale=0.25)
+    dma("s", [(T.mu[:, 0:NH], b("t32", 0, NH))])
+    ts(b("t32", NH, NB), b("acc", NB + NH), 0.25, A.mult, 0.0, A.max)
+    dma("y", [(T.mu[:, NH:NB], b("t32", NH, NB))])
+    act(b("t32", NB), P(5, 0, V - NB), F.Relu, scale=0.25)
+    dma("s", [(T.mu[:, NB:V], b("t32", NB))])
     for tok in ends:
         wait("g", tok)
     for s, n in cnt.items():

from concourse.bass import DstId, RemoteDMATransfer
from concourse.mybir import AluOpType as A, ActivationFunctionType as F

V, X, NR = 768, 128, 8
C = 4 * V
E = (NR - 1) * X
Z = 192
NV = 512
SV = 1024
NS = C + E - SV
NB = 448
LEAD = {1:(4,),-1:(2,)}
NH = 256
QT = 1
CW = 512
QAT = 2
f32, bf, i32, u16, f16 = "float32", "bfloat16", "int32", "uint16", "float16"


def sb(n, d):
    return ("sbuf", [128, n], d)


SCRATCH = {
    "xs": sb(248, i32), "dbt": sb(V, i32), "csh": sb(V, i32), "col": sb(C, bf), "v4": sb(V, f32), "nv": sb(V, f32), "thi": sb(4, i32),
    "io": sb(512, f32), "W32": sb(256, f32), "Wb": sb(256, bf), "Wh": sb(256, f16), "Wq": sb(256, f16), "Un": sb(128, bf), "Gb": sb(2048, bf),
    "Fm": sb(512, bf), "Am": sb(512, f32), "Bm": sb(512, f32), "Em": sb(512, f32), "Rm": sb(128, f32), "B32": sb(128, f32), "Bb": sb(128, bf),
    "one": sb(128, f32), "pi": sb(8, i32), "pp": sb(16, f32), "kq": sb(Z, f32), "cX": sb(NV, bf), "dum": sb(12, f32),
    "Wq32": sb(128, f32), "ch": sb(V, f16), "Un32": sb(128, f32), "Yq": sb(84, f32),
    "clm": sb(C, f32), "lwr": sb(V, f16), "invr": sb(Z + C + E, f32), "Cx": sb(Z + C + E, bf), "S1": sb(Z + V, f32),
    "Dw": sb(C + E, f32), "Lq": sb(V + E, f32), "Lqc": sb(V, f16), "p1h": sb(V, f16), "nH": sb(V, f32), "K": sb(V, bf),
    "rh": sb(C, f16), "r32": sb(C - 4 * NV, f32), "nD": sb(V, bf), "df": sb(E, bf), "z32": sb(Z + C, f32), "zb": sb(C, bf),
    "c0": sb(C + E, bf), "Tw": sb(V + E, bf), "Ts": sb(V, bf), "t32": sb(V, f32), "wa": sb(C + E, f32), "wb": sb(C + E, f32),
    "za": sb(V, bf), "z2": sb(V, bf), "nvt": sb(Z, bf), "a12": sb(2 * Z, bf), "aw": sb(C, bf), "blk": sb(2 * V, bf), "eff": sb(Z, bf),
    "sA": sb(E, f16), "sB": sb(E, f16), "sC": sb(E, bf), "sD": sb(E, bf), "lA": sb(E, f16), "lB": sb(E, f16),
    "ia": sb(248, i32), "ib": sb(248, i32), "ic": sb(248, i32), "fa": sb(248, f32), "fb": sb(248, f32), "fc": sb(Z, f32),
    "qu": sb(248, u16), "xbu": sb(56, u16), "atu": sb(Z, u16), "sigu": sb(Z, u16), "invu": sb(248, u16), "bsl": sb(56, u16), "plu": sb(NB // 4, u16),
    "mk": sb(96, f32), "asku": sb(48, u16), "qbu": sb(48, u16), "lvu": sb(48, u16), "blu": sb(96, u16), "L96": sb(96, f32), "lw": sb(48, i32),
    "X0": sb(144, f32), "X1": sb(240, f32), "thr": sb(96, f32), "km": sb(48, f32), "Y": sb(120, f32), "Yu": sb(120, u16), "sw": sb(96, f32),
    "of": sb(84, f32), "ofu": sb(84, u16), "vs": sb(2 * Z, f32), "vi": sb(2 * Z, f32), "vc": sb(2 * Z, bf), "cp": sb(2 * Z, f32),
    "x1": sb(2 * Z, f32), "x2": sb(2 * Z, f32), "nS": sb(Z, f32),
}
for _b in range(8):
    SCRATCH["P%d" % _b] = ("psum", [128, 512], f32)
ALIAS = {"sigr": ("z32", Z + C), "msg": ("blk", V), "PL": ("wb", 2048), "s32a": ("Lq", E), "s32b": ("Dw", E), "acc": ("r32", 2 * NB)}
NX = 10
SEMAPHORES = (["qv", "qs", "qt", "qg"] + ["ar%d" % x for x in range(NX)] + ["br%d" % x for x in range(NX)] + ["ls%d" % x for x in range(NX)]
              + ["d%d" % x for x in range(30)])


def b(name, c0=0, c1=None, st=1, p=None):
    if name in ALIAS:
        return (ALIAS[name][0], c0, ALIAS[name][1] if c1 is None else c1, st, p, None)
    return (name, c0, SCRATCH[name][1][1] if c1 is None else c1, st, p, None)


def ind(win, off):
    return win[:5] + (off,)


def pieces(*cuts):
    return list(zip(cuts, cuts[1:]))


def rank_program(g, core, T, topo):
    rank = T.rank_of(core)
    if rank is None:
        return
    eng = {"v": g.vector, "s": g.scalar, "t": g.tensor, "g": g, "y": g.sync}
    cnt = {"qv": 0, "qs": 0, "qt": 0, "qg": 0}
    seen = {q: {} for q in eng}
    clock = {}
    hist = {}
    nd = [0]
    ends = []

    def ap(o):
        if not isinstance(o, tuple):
            return o
        ps = slice(None) if o[4] is None else slice(*o[4])
        a = T[o[0]][ps, o[1]:o[2]] if o[3] == 1 else T[o[0]][ps, o[1]:o[2]:o[3]]
        return a if o[5] is None else a.indirect(ap(o[5]))

    def wait(q, tok):
        if seen[q].get(tok[0], 0) >= tok[1]:
            return
        eng[q].wait_ge(T.sem[tok[0]], tok[1])
        seen[q][tok[0]] = tok[1]
        for s, n in clock.get(tok, {}).items():
            if seen[q].get(s, 0) < n:
                seen[q][s] = n

    def span(o):
        return (0, 512, 1) if SCRATCH[o[0]][0] == "psum" else (o[1], o[2], o[3])

    def deps(q, cq, reads, writes):
        need = {}
        for o, wr in [(o, False) for o in reads] + [(o, True) for o in writes]:
            lo, hi, st = span(o)
            ps = SCRATCH[o[0]][0] == "psum"
            for c0, c1, s1, w, qq, tok in hist.get(o[0], []):
                if c0 >= hi or lo >= c1 or not (w or wr or (ps and qq != cq)):
                    continue
                if qq is not None and cq is not None:
                    if qq == cq == "t":
                        continue
                    if st == s1 and (lo - c0) % st:
                        continue
                need[tok[0]] = max(need.get(tok[0], 0), tok[1])
        for s, n in need.items():
            wait(q, (s, n))

    def note(q, cq, reads, writes, tok):
        clock[tok] = dict(seen[q])
        for o in writes:
            hist.setdefault(o[0], []).append(span(o) + (True, cq, tok))
        for o in reads:
            hist.setdefault(o[0], []).append(span(o) + (False, cq, tok))

    def emit(q, fn, out, ins):
        reads = [o for o in ins if isinstance(o, tuple)]
        reads += [o[5] for o in reads + [out] if o[5] is not None]
        deps(q, q, reads, [out])
        s = "q" + q
        cnt[s] += 1
        fn().then_inc(T.sem[s], 1)
        note(q, q, reads, [out], (s, cnt[s]))

    def cp(o, i):
        emit("v", lambda: g.vector.tensor_copy(ap(o), ap(i)), o, [i])

    def tt(o, x, y, op):
        emit("v", lambda: g.vector.tensor_tensor(ap(o), ap(x), ap(y), op), o, [x, y])

    def ts(o, x, s1, op0, s2=None, op1=None):
        if op1 is None:
            emit("v", lambda: g.vector.tensor_scalar(ap(o), ap(x), ap(s1), None, op0), o, [x, s1])
        else:
            emit("v", lambda: g.vector.tensor_scalar(ap(o), ap(x), ap(s1), ap(s2), op0, op1), o, [x, s1, s2])

    def ms(o, c):
        emit("v", lambda: g.vector.memset(ap(o), c), o, [])

    def act(o, i, fn=F.Identity, bias=None, scale=None):
        kw = {}
        if bias is not None:
            kw["bias"] = ap(bias)
        if scale is not None:
            kw["scale"] = scale
        emit("s", lambda: g.scalar.activation(ap(o), ap(i), fn, **kw), o, [i, bias])

    def mm(o, l, r, start, stop):
        emit("t", lambda: g.tensor.matmul(ap(o), ap(l), ap(r), start, stop), o, [l, r])

    def iota(o, pat, base, cm):
        if SCRATCH[o[0]][2] == i32:
            emit("g", lambda: g.iota(ap(o), pat, base, cm), o, [])
        else:
            emit("g", lambda: g.iota(ap(o), pat, base, cm, allow_small_or_imprecise_dtypes=True), o, [])

    def asel(o, i, pat, base, cm, op=A.is_equal):
        emit("g", lambda: g.affine_select(ap(o), ap(i), pat, op, 0.0, base, cm), o, [i])

    def dma(q, pairs):
        s = "d%d" % nd[0]
        nd[0] += 1
        rd = [i for o, i in pairs if isinstance(i, tuple)]
        wr = [o for o, i in pairs if isinstance(o, tuple)]
        deps(q, None, rd, wr)
        for o, i in pairs:
            eng[q].dma_start(ap(o), ap(i)).then_inc(T.sem[s], 16)
        tok = (s, 16 * len(pairs))
        note(q, None, rd, wr, tok)
        ends.append(tok)

    def plan(r, sign):
        c = T.cores[r]
        dst = [(r + sign * (j + 1)) % NR for j in range(NR - 1)]
        near = [j for j in range(NR - 1) if topo.chip(T.cores[dst[j]]) == topo.chip(c)]
        calls = []
        lead = [EARLY[i:j] for i, j in pieces(0, *LEAD[sign])]
        for part in lead + [[j for j in range(NR - 1) if j not in sum(lead, [])]]:
            far = [j for j in part if j not in near]
            en = topo.engines(c, T.cores[dst[far[0]]])
            w = len(en) // len(far)
            row = [(j, dst[j], sum(1 << e for e in en[i * w:(i + 1) * w])) for i, j in enumerate(far)]
            for j in part:
                if j in near:
                    row.append((j, dst[j], sum(1 << e for e in topo.engines(c, T.cores[dst[j]]) if e not in en)))
            calls.append(row)
        return calls

    EARLY = [j for j in range(NR - 1) if all(topo.chip(T.cores[(r + s * (j + 1)) % NR]) != topo.chip(T.cores[r]) for r in range(NR) for s in (1, -1))][:4]
    E0, E1 = EARLY[0] * X, (EARLY[-1] + 1) * X
    LATE = [(E1, E), (0, E0)]
    nx = [0]
    landed = [None]

    def exchange(sign, src, land, l0, make, between=None):
        x = nx[0]
        nx[0] += 1
        sent = 0
        cuts = [E0 + X * i for i in (0,) + LEAD[sign]]
        for n, row in enumerate(plan(rank, sign)):
            last = n == len(LEAD[sign])
            cols = [(cuts[-1], E), (0, E0)] if last else [pieces(*cuts)[n]]
            sem = "ab"[last] + "r%d" % x
            if last and between:
                between()
            for c0, c1 in cols:
                make(c0, c1)
            deps("g", None, [b(src, c0, c1) for c0, c1 in cols], [])
            trs = []
            for j, d, m in row:
                rid, pid, _ = topo.addr(T.cores[d])
                trs.append(RemoteDMATransfer(dst_ids=[DstId(rid=rid, pnc=pid)], dma_engine_mask=m, remote_sem=T.sem[sem],
                                             src=ap(b(src, j * X, (j + 1) * X)), dst=T[land][:, l0 + j * X:l0 + (j + 1) * X]))
                sent += bin(m).count("1")
            g.remote_dma_fused(trs, local_sem=T.sem["ls%d" % x])
            tok = (sem, sum(bin(m).count("1") for r in range(NR) if r != rank
                            for call in (plan(r, sign)[-1:] if last else plan(r, sign)[:-1]) for j, d, m in call if d == rank))
            clock[tok] = {}
            landed[0] = tok
            for c0, c1 in cols:
                hist.setdefault(land, []).append((l0 + c0, l0 + c1, 1, True, None, tok))
        note("g", None, [b(src)], [], ("ls%d" % x, sent))
        ends.append(("ls%d" % x, sent))

    def mat(name, kind):
        c = {"I": 0, "D": 16, "U": 112}[kind]
        return b(name, c, c + 128)

    def m4(name, h):
        return b(name, 128 * h, 128 * h + 128)

    def col(j):
        return b("pp", j, j + 1)

    def P(k, c0=0, c1=512, st=1):
        return b("P%d" % k, c0, c1, st)

    def gat(win, lst, c0, c1):
        return ind(win, b(lst, c0 // 16, c1 // 16))

    ROW, ROW2 = (0, 128, 18), (14, 113, 14)
    vb = ((0, NV), (NV, V))
    GP = [[256, 16], [-ROW[2], 8], [-256, 16]]

    def spread(dst, src):
        dma("y", [(b(dst, Z, None, 1, ROW), src)])

    def round_matrices(t):
        o = 4 * (3 - t)
        for h in range(4):
            asel(m4("Am", h), b("one"), [[-16, 8], [256, 4], [-1, 4]], -o - 256 * h, 1)
            asel(m4("Bm", h), b("one"), [[-16, 8], [256, 4], [0, 4]], -o - 256 * h, 1)
        asel(b("Rm"), b("one"), [[-16, 8], [0, 16]], -o, 1)

    dma("y", [(b("xs", Z, 248), T.xpt[:])])
    dma("s", [(b("dbt"), T.debt[:])])
    iota(b("pi", 0, 1), [[0, 1]], 0, 1)
    iota(b("io"), [[1, 512]], 0, 0)
    ms(b("fb"), 0.0)
    dma("y", [(b("wb", 0, None, 1, ROW2), b("fb"))])
    dma("y", [(b("xs", 0, Z), T.sig[:])])
    dma("y", [(b("invr", Z, None, 1, ROW), b("fb"))])
    dma("y", [(b("col"), T.coll[:])])
    dma("y", [(b("csh"), T.cash[:]), (b("thi", 0, 1), T.th[:])])
    for c0 in range(0, V, Z):
        act(b("K", c0, c0 + Z), b("fb", 0, Z), F.Silu)
    ms(b("W32"), 1.0)
    ms(b("one"), 1.0)
    ms(b("B32"), 4.0)
    asel(b("W32"), b("W32"), [[0, 2], [-1, 128]], 0, 1)
    p0 = b("pi", 0, 1)
    ts(b("pi", 1, 2), p0, 3, A.bitwise_and)
    ts(b("pi", 2, 3), p0, 2, A.arith_shift_right, 3, A.bitwise_and)
    ts(b("pi", 3, 4), p0, 15, A.bitwise_and)
    cp(b("pp", 1, 4), b("pi", 1, 4))
    for t in range(2):
        ts(col(9 + t), col(2), 16.0, A.mult, 13.0 - 4 * t, A.add)
    ts(col(5), col(3), -float(Z), A.add, 1.0 / 8192, A.mult)
    ts(col(4), col(1), 192.0, A.mult)
    ts(col(8), col(1), 192.0, A.mult, col(2), A.add)
    for t in range(2):
        ts(col(11 + t), col(8), 768.0 * (3 - t), A.add)
    for c0, c1 in pieces(NS - E, NS - E + 512, NS):
        act(b("z32", c0, c1), b("io", 0, c1 - c0), bias=float(64 + SV + c0))
    iota(b("z32", 1024, NS - E), [[1, NS - E - 1024]], 64 + SV + 1024, 0)
    for c0, c1 in pieces(0, 512, 1024):
        ts(b("z32", c0, c1), b("io"), float(64 + SV + c0), A.add)
    ts(b("ic", Z, 248), b("xs", Z, 248), 2, A.arith_shift_right)
    cp(b("xbu"), b("ic", Z, 248))

    def places(c0, c1):
        ts(b("ia", c0, c1), b("xs", c0, c1), 4, A.arith_shift_right)
        ts(b("ib", c0, c1), b("xs", c0, c1), 248.0, A.mult)
        ts(b("ia", c0, c1), b("ia", c0, c1), -3967.0, A.mult)
        tt(b("ia", c0, c1), b("ia", c0, c1), b("ib", c0, c1), A.add)
        cp(b("qu", c0, c1), b("ia", c0, c1))
    exchange(1, "sA", "lA", 0, lambda c0, c1: ts(b("sA", c0, c1), gat(b("dbt"), "xbu", c0, c1), -512.0, A.add), lambda: places(Z, 248))
    act(ind(b("wb"), b("qu", Z, 248)), b("z32", NS - E, NS), F.Silu)
    places(SV // 16, Z)
    act(ind(b("wb"), b("qu", SV // 16, Z)), b("z32", 0, NS - E), F.Silu)
    iota(b("cX"), [[0, NV]], -128, 0)
    asel(b("B32"), b("B32"), [[-16, 8], [0, 16]], 0, 1, A.is_ge)
    asel(b("B32"), b("B32"), [[16, 8], [0, 16]], 15, -1, A.is_ge)
    for h in range(4):
        asel(m4("Fm", h), b("B32"), [[0, 8], [1, 4], [0, 4]], -h, 0)
    asel(b("Rm"), b("one"), [[-16, 8], [0, 4], [-4, 4]], 0, 1, A.is_ge)
    asel(b("Rm"), b("Rm"), [[16, 8], [0, 4], [4, 4]], 3, -1, A.is_ge)
    for h in range(4):
        asel(m4("Em", h), b("Rm"), [[0, 8], [1, 4], [0, 4]], -h, 0)
    iota(b("kq"), [[1, 4], [0, 48]], 0, 0)
    round_matrices(0)
    iota(b("z32", NS), [[0, Z + C - NS]], 0, 0)
    act(b("Un32"), mat("W32", "U"), scale=-1.0)
    act(b("Wq32"), mat("W32", "I"), scale=0.25)
    cp(b("Wh"), b("W32"))
    cp(b("Wb"), b("W32"))
    ts(b("Wq"), b("W32"), 0.25, A.mult)
    ts(b("Un"), mat("W32", "U"), -1.0, A.mult)
    places(0, SV // 16)
    ts(b("ic", 0, Z), b("xs", 0, Z), 2, A.arith_shift_right)
    ts(b("ib", 0, Z), b("xs", 0, Z), -2304.0, A.add)
    ts(b("ch"), b("csh"), -512.0, A.add)
    tt(b("ib", 0, Z), b("ib", 0, Z), b("ic", 0, Z), A.max)
    ts(b("Lq", 0, V), b("dbt"), 0.25, A.mult)
    cp(b("atu"), b("ib", 0, Z))
    for c0 in range(0, SV, 512):
        n = min(512, SV - c0)
        ts(gat(b("invr", Z), "qu", c0, c0 + n), b("io", 0, n), 1.0, A.mult, float(64 + c0), A.add)
    dma("y", [(b("fa"), b("invr", Z, None, 1, ROW))])
    dma("y", [(b("fb"), b("wb", 0, None, 1, ROW2))])
    dma("y", [(b("v4"), T.val[:]), (b("nv", 0, None, 1, (0, 112)), T.val[16:128, :]), (b("nv", 0, None, 1, (112, 128)), T.val[0:16, :])])
    dma("y", [(b("aw", c0, c0 + V), b("K")) for c0 in range(0, C, V)])

    for j in range(2):
        mm(P(4 + j, 0, 384), mat("Wh", "I"), b("ch", 384 * j, 384 * j + 384), True, False)
    for i, (a0, a1) in enumerate(vb):
        mm(P(6 + i, 0, a1 - a0), mat("Wh", "I"), b("ch", a0, a1), True, False)
        for k in range(4):
            if i == 0:
                mm(P(6, 0, NV), b("Un"), b("cX"), False, False)
            mm(P(6 + i, 0, a1 - a0), mat("Wb", "I"), b("col", 4 * a0 + k, 4 * a1, 4), False, k == 3)
    for k, (c0, c1) in enumerate([(E0, E1)] + LATE):
        mm(P(k, 0, c1 - c0), mat("Wq", "U"), b("lA", c0, c1), True, True)
        ts(b("Lq", V + c0, V + c1), P(k, 0, c1 - c0), 128.0, A.add)
    for j, (c0, c1) in enumerate(pieces(0, 768, 1536, 2560, C)):
        tt(b("rh", c0, c1), gat(b("Lq"), "atu", c0, c1), b("col", c0, c1), A.max)
        for k in range(4):
            mm(P(4 + j // 2, c0 // 4 % 384, (c1 // 4 - 1) % 384 + 1), mat("Wh", "I"), b("rh", c0 + k, c1, 4), False, j % 2 == 1 and k == 3)
        if j == 1:
            act(b("S1", Z, Z + 384), P(4, 0, 384))
        if j == QT:
            mm(P(2, 0, 248), mat("W32", "I"), b("fa"), True, False)
            mm(P(2, 0, 248), mat("W32", "I"), b("fb"), False, True)
        if j == QAT:
            ts(b("qu"), P(2, 0, 248), -63.75, A.add, C - 0.75, A.min)
    cp(b("S1", Z + 384), P(5, 0, 384))

    def open_sums():
        for j, (c0, c1) in enumerate(vb):
            mm(P(4 + j, 0, c1 - c0), mat("Wh", "D"), b("ch", c0, c1), True, False)
            mm(P(4 + j, 0, c1 - c0), mat("Wb", "D"), b("K", c0, c1), False, False)

    def first_lists():
        act(b("Cx", Z, Z + 1536), gat(b("col"), "qu", 0, 1536), scale=-1.0)
        act(b("fa"), P(2, 0, 248))
        act(b("Cx", Z + 1536, Z + C), gat(b("col"), "qu", 1536, C), scale=-1.0)
        ts(b("Lqc"), b("dbt"), -512.0, A.add)
        for j in range(2):
            tt(b("p1h", 384 * j, 384 * j + 384), P(4 + j, 0, 384), b("Lqc", 384 * j, 384 * j + 384), A.min)
        for j, (c0, c1) in enumerate(vb):
            tt(b("ch", c0, c1), P(6 + j, 0, c1 - c0), b("Lqc", c0, c1), A.subtract)
        if CW:
            act(b("Cx", Z + C, Z + C + CW), gat(b("col"), "qu", C, C + CW), scale=-1.0)
        if CW < E:
            ts(b("Cx", Z + C + CW), gat(b("col"), "qu", C + CW, C + E), -1.0, A.mult)
        ts(b("fc"), b("xs", 0, Z), 64.0, A.add)

    def swap_lists():
        for c0 in range(36, 84, 12):
            tt(b("of", c0, c0 + 12), P(3, 0, 12), b("Yq", c0, c0 + 12), A.min)
        ts(b("ofu", 36), b("of", 36), 8192.0, A.mult, float(Z), A.add)

    def swaps():
        for e in range(2):
            act(ind(b("sigr"), b("ofu", 12 + 12 * e, 24 + 12 * e)), b("vs", Z - Z * e, 2 * Z - Z * e), F.Silu)
        dma("y", [(b("fc"), b("sigr", Z, None, 1, ROW))])
        for e in range(2):
            act(ind(b("invr"), b("ofu", 60 + 12 * e, 72 + 12 * e)), b("vi", Z - Z * e, 2 * Z - Z * e), F.Silu)
        dma("y", [(b("fa"), b("invr", Z, None, 1, ROW))])
        for j in range(2):
            mm(P(6 + j, 0, 384), mat("W32", "I"), b("S1", Z + 384 * j, Z + 384 * j + 384), True, True)
            tt(b("p1h", 384 * j, 384 * j + 384), P(6 + j, 0, 384), b("Lqc", 384 * j, 384 * j + 384), A.min)
        open_sums()
        for e in range(2):
            cp(ind(b("Cx"), b("ofu", 36 + 12 * e, 48 + 12 * e)), b("vc", Z - Z * e, 2 * Z - Z * e))

    def clear2(t):
        close = t == 2
        o = 4 * (3 - t)
        exchange(1, "sB", "lB", 0, lambda c0, c1: tt(b("sB", c0, c1), gat(b("S1", Z), "xbu", c0, c1), b("sA", c0, c1), A.min), swap_lists if t else None)
        if t == 0:
            iota(b("Gb"), [[0, 2048]], 1, 0)
            asel(b("Gb"), b("Gb"), GP, 0, 1)
            first_lists()
            spread("sigr", b("fc"))
            spread("invr", b("fa"))
        else:
            swaps()
        if t == 1:
            round_matrices(1)
            iota(b("aw", 12, C, 16), [[0, Z]], 0, 0)
        (a0, a1), (b0, b1) = LATE
        wire = [(1, 0, E0, E1, "I", "U"), (2, 0, E0, E1, "D", "I"),
                (0, 0, a0, a1, "I", "U"), (6, 0, b0, b1, "I", "U"), (3, 0, a0, a1, "D", "I"), (3, a1 - a0, b0, b1, "D", "I")]

        def over(n):
            k, at, c0, c1, kind, _ = wire[n]
            mm(P(k, at, at + c1 - c0), mat("Wb", kind), b("Cx", Z + C + c0, Z + C + c1), at == 0, False)

        def paid(n):
            k, at, c0, c1, _, kind = wire[n]
            mm(P(k, at, at + c1 - c0), mat("Wq", kind), b("lB", c0, c1), False, n != 4)
            return P(k, at, at + c1 - c0)
        mm(P(0, 0, 384), mat("Wq", "I"), b("p1h", 0, 384), True, False)
        mm(P(0, 0, 384), b("Un"), b("cX", 0, 384), False, True)
        if t == 0:
            open_sums()
        for k in (2, 3, 6, 7):
            mm(P(k, 0, 384), mat("Wq", "I"), b("p1h", 384), True, False)
        for l, k in enumerate((2, 3, 6, 7)):
            tt(b("Dw", l, 1536, 4), P(0, 0, 384), b("Cx", Z + l, Z + 1536, 4), A.add)
            mm(P(k, 0, 384), mat("Wb", "I"), b("Cx", Z + 1536 + l, Z + C, 4), False, True)
            act(b("Dw", 1536 + l, C, 4), P(k, 0, 384), bias=128.0)
        for n in (0, 1, 4, 5):
            over(n)
        ts(b("Dw", C + E0, C + E1), paid(0), 128.0, A.add)
        over(3)
        over(2)
        paid(1)
        ts(b("sigu"), b("fc"), -63.75, A.add)
        ts(b("Dw", C + a0, C + a1), paid(2), 128.0, A.add)
        act(b("Dw", C + b0, C + b1), paid(3), bias=128.0)
        mine, theirs = pieces(0, 512, 1280, 4 * NV - 256, 4 * NV), pieces(0, 128, 384, 704, C - 4 * NV)
        for c0, c1 in mine:
            ts(b("rh", c0, c1), gat(b("Dw"), "sigu", c0, c1), 0.0, A.max, -128.0, A.add)
        for j, (c0, c1) in enumerate(theirs):
            act(b("r32", c0, c1), gat(b("Dw"), "sigu", 4 * NV + c0, 4 * NV + c1), F.Relu)
        for e, j in ((1, 0), (1, 1), (0, 0), (1, 2), (1, 3), (0, 1), (0, 2), (0, 3)):
            c0, c1 = (mine, theirs)[e][j]
            for k in range(4):
                mm(P(4 + e, c0 // 4, c1 // 4), mat(("Wh", "W32")[e], "D"), b(("rh", "r32")[e], c0 + k, c1, 4), False, j == 3 and k == 3)
            if (e, j) == (1, 1):
                mm(P(7, 0, 56), mat("W32", "D"), b("fa", Z, 248), True, True)
        paid(4)
        paid(5)
        ts(b("ib", 0, 56), P(7, 0, 56), 0.25, A.mult, -16.375, A.add)
        cp(b("bsl"), b("ib", 0, 56))
        for k in range(0 if close else 4):
            ts(b("msg", k, NV, 4), b("rh", o + k, 4 * NV, 16), -128.0, A.is_gt)
        sg = -1.0 if close else 1.0

        def over_there():
            for k, at, c0, c1, _, _ in wire[4:]:
                act(b("df", c0, c1), P(k, at, at + c1 - c0), bias=128.0 * sg, scale=sg)
        act(b("df", E0, E1), P(2, 0, E1 - E0), bias=128.0 * sg, scale=sg)
        if close:
            over_there()
            for j in (1, 0):
                tt(b("t32", *vb[j]), P(4 + j, 0, vb[j][1] - vb[j][0]), b("nv", *vb[j]), A.max)
            exchange(-1, "s32a", "wa", C, lambda c0, c1: tt(b("s32a", c0, c1), gat(b("t32"), "bsl", c0, c1), b("df", c0, c1), A.max))
            for c0, c1, k in ((NV, V, 2), (0, NV, 3)):
                mm(P(k, 0, c1 - c0), b("Wq32"), b("v4", c0, c1), True, True)
            for j in range(2):
                act(b("nD", *vb[j]), P(4 + j, 0, vb[j][1] - vb[j][0]), F.Relu, bias=4096.0, scale=131072.0)
        else:
            act(b("nD", NV), P(5, 0, V - NV), F.Relu, bias=512.0, scale=16384.0)
            ts(b("nD", 0, NV), P(4, 0, NV), 0.0, A.is_ge, 512.0, A.mult)
            over_there()
            exchange(-1, "sC", "c0", C, lambda c0, c1: tt(b("sC", c0, c1), gat(b("nD"), "bsl", c0, c1), b("df", c0, c1), A.is_lt))
        if t == 0:
            ts(col(6), b("thi", 0, 1), -1.0, A.mult, 16.0, A.add)
            ts(b("dum"), b("io", 0, Z, 16), 1.0 / 8192, A.mult, col(5), A.add)
            iota(b("clm"), [[1, 16], [16, Z]], 64, 0)
        if t == 1:
            for l in range(4):
                for r in range(4):
                    asel(m4("PL", 4 * l + r), b("one"), [[-16, 8], [256, 4], [-4, 4]], -l - 256 * r, 1)
        if not close:
            wiring_sums(t)
        mm(P(6, 0, V - NV), mat("Wb", "U"), b("nD", NV), True, True)
        for j, (c0, c1) in enumerate(pieces(0, 512, 1024, 1536, 4 * NV)):
            if j == 2 and not close:
                wiring(t)
            mm(P(j % 2, 0, c1 - c0), mat("Wh", "I"), b("rh", c0, c1), True, False)
            for k in range(4):
                mm(P(j % 2, k, c1 - c0, 4), b("Un"), b("nD", c0 // 4, c1 // 4), False, k == 3)
            if close:
                act(b("c0", c0, c1), P(j % 2, 0, c1 - c0), F.Relu, bias=128.0 * 8192, scale=8192.0)
            else:
                act(b("c0", c0, c1), P(j % 2, 0, c1 - c0), F.Sign, bias=128.0 - 1.0 / 32)
        if not close:
            barred(t)
            for i in range(16):
                mm(P(3, 0, 48), m4("Gb", i), b("lwr", i, V, 16), i == 0, i == 15)
        steps = [] if close else least()
        for k in range(4):
            for step in steps[k:k + 1]:
                step()
            tt(b("c0", 4 * NV + k, C, 4), b("r32", k, None, 4), P(6, 0, V - NV), A.is_gt)
        for step in steps[4:5]:
            step()
        ts(b("invu"), b("fa"), -63.75, A.add)

    def wiring_sums(t):
        o = 4 * (3 - t)
        for h in range(4):
            mm(P(7, 0, 48), m4("Bm", h), b("fa", h, Z, 4), h == 0, h == 3)
        for k in range(4):
            act(b("msg", NV + k, V, 4), b("r32", o + k, None, 16), F.Sign)
        act(b("x1", 0, Z), b("io", 0, Z), bias=-(o + 65.5), scale=-16.0)
        act(b("X0", 0, 48), b("io", 0, Z, 4), bias=col(11 + t))
        act(b("thr", 0, 48), b("io", 0, Z, 4), bias=col(9 + t), scale=16.0)
        act(b("thr", 48, 96), b("thr", 0, 48), bias=-1.0)

    def barred(t):
        mm(P(3, 64, 64 + Z), b("Rm"), b("fa", 0, Z), True, True)
        mm(P(3, 64 + Z, 64 + 2 * Z), b("Rm"), b("fa", 0, Z), True, False)
        mm(P(3, 64 + Z, 64 + 2 * Z), mat("W32", "I"), b("x1", 0, Z), False, True)
        act(b("x2", 0, Z), P(3, 64 + Z, 64 + 2 * Z), F.Abs)
        act(b("a12", 0, Z), P(3, 64, 64 + Z), F.Relu, bias=-128.0 * (C + 63.5), scale=128.0)
        act(b("a12", Z), b("x2", 0, Z), F.Relu, bias=256.0, scale=-128.0)

    def wiring(t):
        for j, src in enumerate(("fc", "fa")):
            for h in range(4):
                mm(P(4, 48 * j, 48 * j + 48), m4("Am", h), b(src, h, Z, 4), h == 0, h == 3)
        mm(P(2, 0, Z), mat("W32", "I"), b("kq"), True, False)
        for k in range(4):
            for h in range(4):
                mm(P(2, 48 * k, 48 * k + 48), m4("Fm", h), b("msg", 4 * h + k, V, 16), False, k == 3 and h == 3)
        ts(b("ia", 0, 48), P(7, 0, 48), 0.25, A.mult, -16.375, A.add)
        ts(b("ia", 48, 96), P(7, 0, 48), 0.0625, A.mult, -4.46875, A.add)
        ts(b("ib", 0, 48), b("ia", 0, 48), 768.0, A.mult, col(4), A.add)
        ts(b("ib", 48, 96), b("ia", 48, 96), -3071.0, A.mult)
        ts(b("X1", 192, 240), b("ia", 0, 48), 4.0, A.mult)
        tt(b("ib", 0, 48), b("ib", 0, 48), b("ib", 48, 96), A.add)
        ts(b("qbu"), b("ib", 0, 48), float(C - 1), A.min)
        ts(b("X0", 48, 96), b("ib", 0, 48), float(C - 1), A.min)
        ts(b("lwr"), ind(b("sigr", Z), b("qbu")), -64.0 - 2048, A.add)
        ts(b("lvu"), P(4, 0, 48), -63.75, A.add)
        ts(b("ic", 0, 48), P(4, 48, 96), 0.25, A.mult, -16.375, A.add)
        ts(b("ic", 48, 96), P(4, 48, 96), -2368.0, A.add)
        cp(b("X0", 96, 144), b("lvu"))
        tt(b("ic", 0, 48), b("ic", 0, 48), b("ic", 48, 96), A.max)
        cp(b("asku"), b("ic", 0, 48))

    def least():
        return [lambda: cp(b("mk", 0, 96), P(2, 0, 96)),
                lambda: tt(b("mk", 0, 96), P(2, 96, Z), b("mk", 0, 96), A.min),
                lambda: tt(b("ia", 0, 48), b("mk", 0, 48), b("mk", 48, 96), A.min),
                lambda: ts(b("ia", 0, 48), b("ia", 0, 48), 3, A.bitwise_and),
                lambda: ts(b("km"), b("ia", 0, 48), col(1), A.is_equal)]

    def choices(t):
        for j in range(3):
            tt(b("X1", 48 * j, 48 * j + 48), b("X0", 48 * j, 48 * j + 48), b("km"), A.mult)
        ts(b("lw"), P(3, 0, 48), 2048.0, A.add)
        tt(b("L96", 0, 48), b("X0", 96, 144), b("thr", 0, 48), A.min)
        tt(b("X1", 144, 192), b("lw"), b("km"), A.mult)
        for r in range(4):
            mm(P(0, 0, 60), m4("Em", r), b("X1", r, 240, 4), r == 0, r == 3)
        tt(b("sw", 0, 48), b("lw"), b("thr", 48, 96), A.is_equal)
        tt(b("sw", 48, 96), b("X1", 192, 240), b("lw"), A.subtract)
        tt(b("sw", 0, 48), b("sw", 0, 48), b("sw", 48, 96), A.mult)
        tt(b("sw", 0, 48), b("sw", 0, 48), b("lw"), A.add)
        tt(b("L96", 48, 96), b("sw", 0, 48), b("thr", 0, 48), A.min)
        cp(b("Yu", 0, 48), P(0, 0, 48))
        act(b("cp"), ind(b("Cx", Z), b("Yu", 24, 48)), scale=-1.0)
        ts(b("ib", 24, 48), P(0, 24, 48), 0.25, A.mult, -0.375, A.add)
        ts(b("ic", 24, 48), P(0, 24, 48), -2304.0, A.add)
        ts(b("ib", 0, 24), P(0, 24, 48), 0.0625, A.mult, -0.46875, A.add)
        ts(b("ic", 0, 24), P(0, 24, 48), 248.0, A.mult)
        ts(b("Y", 72, 84), P(0, 48, 60), 0.0625, A.mult, float(V - 1), A.min)
        tt(b("Y", 84, 108), b("ib", 24, 48), b("ic", 24, 48), A.max)
        ts(b("ib", 0, 24), b("ib", 0, 24), -3967.0, A.mult)
        tt(b("Y", 108, 120), b("ib", 24, 36), b("ic", 24, 36), A.max)
        tt(b("Y", 48, 72), b("ib", 0, 24), b("ic", 0, 24), A.add)
        cp(b("blu"), b("L96"))
        cp(b("Yu", 48), b("Y", 48))
        tt(b("x1"), ind(b("Lq"), b("Yu", 96, 120)), b("cp"), A.max)
        tt(b("x2"), ind(b("Lq"), b("Yu", 84, 108)), b("cp"), A.max)
        tt(b("x1"), b("x1"), b("x2"), A.subtract)
        tt(b("nS"), ind(b("S1", Z), b("Yu", 72, 84)), b("x1", Z), A.add)
        for l in range(4):
            act(b("za", l, V, 4), b("zb", 4 * (3 - t) + l, C, 16))
        act(b("Yq", 12, 60), P(0, 0, 48), scale=1.0 / 8192)
        act(b("Yq", 60), b("Y", 48, 72), scale=1.0 / 8192)
        act(b("Yq", 0, 12), b("Y", 72, 84), scale=1.0 / 8192)
        act(b("vc"), b("cp"), scale=-1.0)
        act(P(1, 0, Z), b("x1", 0, Z), bias=56.0)

    for t in range(2):
        o = 4 * (3 - t)
        clear2(t)
        bank = ((4, 6), (5, 0))
        for j, (c0, c1) in enumerate(pieces(0, 512, 1024, 1280, 1536)):
            ts(b("zb", c0, c1), gat(b("c0"), "invu", c0, c1), 0.0, A.max)
            act(b("zb", 1536 + c0, 1536 + c1), gat(b("c0"), "invu", 1536 + c0, 1536 + c1), F.Relu)
            for e in range(2):
                for k in range(4):
                    mm(P(bank[e][j // 3], c0 // 4, c1 // 4), mat("Wb", "D"), b("zb", 1536 * e + c0 + k, 1536 * e + c1, 4), k == 0, k == 3)
        for j, (c0, c1) in enumerate(pieces(0, 320, 384)):
            ts(b("Ts", c0, c1), P(bank[0][j], c0, c1), -1.0, A.mult, -4.0, A.add)
            act(b("Ts", 384 + c0, 384 + c1), P(bank[1][j], c0, c1), bias=-4.0, scale=-1.0)

        def make_d(c0, c1):
            m = c1 if c0 == 0 else (c0 + c1 - (E0 if c1 == E else 0)) // 2
            if m < c1:
                act(b("sD", m, c1), gat(b("Ts"), "bsl", m, c1))
            cp(b("sD", c0, m), gat(b("Ts"), "bsl", c0, m))
        exchange(-1, "sD", "Tw", V, make_d)
        if t == 0:
            act(b("Bb"), b("B32"))
        for j in range(2):
            mm(P(1 + j, 0, 384), mat("Wb", "U"), b("Ts", 384 * j, 384 * j + 384), True, True)
            act(b("Tw", 384 * j, 384 * j + 384), P(1 + j, 0, 384))
        choices(t)
        mm(P(4, 0, Z), mat("Wb", "U"), b("nD", 3 - t, V, 4), True, False)
        mm(P(5, 0, Z), mat("Wb", "I"), b("a12", 0, Z), True, False)
        mm(P(5, 0, Z), mat("Wb", "I"), b("a12", Z), False, False)
        mm(P(3, 0, 12), mat("W32", "I"), b("dum"), True, False)
        cut = pieces(0, 512, V)
        for j, (c0, c1) in enumerate(cut):
            tt(b("z2", c0, c1), gat(b("Tw"), "asku", c0, c1), b("za", c0, c1), A.mult)
            for l in range(4):
                mm(P(4, c0 // 4, c1 // 4), mat("Wb", "I"), b("z2", c0 + l, c1, 4), False, j == 1 and l == 3)
        act(b("vs"), ind(b("sigr", Z), b("Yu", 0, 24)))
        act(b("vi"), ind(b("clm"), b("Yu", 0, 24)))
        if t == 0:
            act(b("nv"), b("nv"), scale=-2.0 ** -12)
        else:
            act(b("v4"), b("v4"), scale=4.0)
        ts(b("nvt"), P(4, 0, Z), col(6), A.is_gt)
        mm(P(5, 0, Z), b("Bb"), b("nvt"), False, True)
        ts(b("aw", o, C, 16), P(5, 0, Z), 30.0, A.is_le)
        for j, (c0, c1) in enumerate(pieces(0, 256, 512, V)):
            act(b("blk", V + c0, V + c1), gat(b("aw"), "blu", V + c0, V + c1))
            cp(b("blk", c0, c1), gat(b("aw"), "blu", c0, c1))
            for e in range(2):
                for k in range(4):
                    mm(P(6, c0 // 4, c1 // 4), mat("Wb", "I"), b("blk", V * e + c0 + k, V * e + c1, 4), e == 0 and k == 0, e == 1 and k == 3)
        tt(b("eff"), P(6, 0, Z), b("aw", o, C, 16), A.is_lt)
        for i in range(16):
            mm(P(3, 0, 12), m4("Gb", i), b("eff", i, Z, 16), False, i == 15)
        act(b("K", 3 - t, V, 4), b("eff"), scale=56.0)
        tt(P(1, Z, 2 * Z), P(1, 0, Z), b("eff"), A.mult)
        tt(b("S1", Z + 3 - t, None, 4), P(1, Z, 2 * Z), b("S1", Z + 3 - t, None, 4), A.add)
        for c0 in range(0, 36, 12):
            tt(b("of", c0, c0 + 12), P(3, 0, 12), b("Yq", c0, c0 + 12), A.min)
        ts(b("ofu", 0, 36), b("of", 0, 36), 8192.0, A.mult, float(Z), A.add)
        cp(ind(b("S1"), b("ofu", 0, 12)), b("nS"))

    clear2(2)
    nb = NB // 16
    for l in range(4):
        for r in range(4):
            mm(P(7, nb * l, nb * l + nb), m4("PL", 4 * l + r), b("fa", r, NB // 4, 4), r == 0, r == 3)
    for j in range(2):
        act(b("S1", Z + vb[j][0], Z + vb[j][1]), P(4 + j, 0, vb[j][1] - vb[j][0]), F.Relu, scale=-1.0)

    def masked(win, banks):
        for (c0, c1, op), p in zip(((NV, V, A.mult), (0, NV, A.min)), banks):
            for k in range(4):
                tt(b(win, 4 * c0 + k, 4 * c1, 4), b("c0", 4 * c0 + k, 4 * c1, 4), P(p, 0, c1 - c0), op)
    masked("wa", (2, 3))
    ts(b("plu"), P(7, 0, 4 * nb), -63.75, A.add)
    act(b("df"), b("s32a"), F.Relu, scale=-2.0 ** 26)

    def sweep32(win, kind, first, done):
        cut = pieces(0, 128, 448, 896, C - 4 * NB)
        for c0, c1 in hb:
            for l in range(4):
                tt(b("acc", NB * (l % 2) + c0, NB * (l % 2) + c1), gat(b(win), "plu", NB * l + c0, NB * l + c1),
                   b(first, c0, c1) if l == 0 else b("acc", NB - NB * (l % 2) + c0, NB - NB * (l % 2) + c1), A.add)
        for j, (c0, c1) in enumerate(cut):
            act(b("z32", c0, c1), gat(b(win), "invu", 4 * NB + c0, 4 * NB + c1))
            for k in range(4):
                mm(P(5, c0 // 4, c1 // 4), mat("W32", kind), b("z32", c0 + k, c1, 4), False, j == 3 and k == 3)
            if j >= 2:
                done(j - 2, *hb[j - 2])
    hb = pieces(0, NH, NB)
    mm(P(5, 0, V - NB), mat("W32", "D"), b("v4", NB), True, False)
    e1 = E0 + X * LEAD[-1][-1]
    m = (e1 + E + E0) // 2
    for c0, c1 in ((E0, e1), (e1, m)):
        ts(b("wa", C + c0, C + c1), b("wa", C + c0, C + c1), -4096.0, A.mult, 0.0, A.max)
    for c0, c1 in ((m, E), (0, E0)):
        if c0 < c1:
            act(b("wa", C + c0, C + c1), b("wa", C + c0, C + c1), F.Relu, scale=-4096.0)
    sweep32("wa", "D", "v4", lambda j, c0, c1: mm(P(6 - 2 * j, c0, c1), mat("W32", "D"), b("acc", NB + c0, NB + c1), True, True))
    act(b("t32", 0, NH), P(6, 0, NH), scale=0.25)
    act(b("t32", NB), P(5, 0, V - NB), scale=0.25)
    ts(b("t32", NH, NB), P(4, NH, NB), 0.25, A.mult)
    exchange(-1, "s32b", "wb", C, lambda c0, c1: tt(b("s32b", c0, c1), gat(b("t32"), "bsl", c0, c1), b("df", c0, c1), A.min))
    for j, (c0, c1) in enumerate(((NV, V), (0, NV))):
        mm(P(j, 0, c1 - c0), mat("W32", "U"), b("t32", c0, c1), True, True)
    masked("wb", (0, 1))
    for k, (c0, c1) in ((6, (0, NB)), (5, (NB, V))):
        mm(P(k, 0, c1 - c0), mat("W32", "I"), b("v4", c0, c1), True, False)
        mm(P(k, 0, c1 - c0), b("Un"), b("nD", c0, c1), False, k == 6)
    act(b("nv", 0, NB), P(6, 0, NB))
    for j in range(2):
        mm(P(2 + j, 0, 384), mat("Wh", "I"), b("Lqc", 384 * j, 384 * j + 384), True, False)
        mm(P(2 + j, 0, 384), b("Un32"), b("S1", Z + 384 * j, Z + 384 * j + 384), False, True)
        act(b("nH", 384 * j, 384 * j + 384), P(2 + j, 0, 384), bias=512.0)
    for tok in ends:
        wait("g", tok)
    wait("y", landed[0])
    dma("y", [(T.pay[:], b("nH"))])
    sweep32("wb", "I", "nv", lambda j, c0, c1: None)
    act(b("t32", 0, NH), b("acc", NB, NB + NH), F.Relu, scale=0.25)
    dma("s", [(T.mu[:, 0:NH], b("t32", 0, NH))])
    ts(b("t32", NH, NB), b("acc", NB + NH), 0.25, A.mult, 0.0, A.max)
    dma("y", [(T.mu[:, NH:NB], b("t32", NH, NB))])
    act(b("t32", NB), P(5, 0, V - NB), F.Relu, scale=0.25)
    dma("s", [(T.mu[:, NB:V], b("t32", NB))])
    for tok in ends:
        wait("g", tok)
    for s, n in cnt.items():
        wait("g", (s, n))
